import numpy as np, ml_dtypes
CORES = [1,5,17,21,33,37,49,53]
N = 8
BF = ml_dtypes.bfloat16
S, L, CAP, RO, KM = 4096, 512, 96, 3, 3967
W = S + RO * CAP
def joined(c, T):
    e = np.add.accumulate(4 + (c & 3), axis=1)
    j = np.minimum(np.sum(e[:, :, None] <= (5 * np.arange(L) + 2)[None, None, :], axis=1), L - 2)
    p = np.take_along_axis(c, j, 1); q = np.take_along_axis(c, j + 1, 1)
    left = np.take_along_axis(T, p[:, None, :], 2)[:, 8:]; right = np.take_along_axis(T, q[:, None, :], 2)[:, :8]
    return p, np.concatenate([left, right], axis=1).astype(np.int64)
def places(z, w, k):
    u = np.sum(z * w[:, :, 0:1], axis=1) & (S - 1); v = np.sum(z * w[:, :, 1:2], axis=1) & (S - 1)
    return (((u * v) >> 5)[:, None, :] + k[:, :, None] * u[:, None, :]) & (S - 1)
def probe(z, w, k, b, U):
    h = places(z, w, k)
    d = np.stack([np.sum(np.abs(np.take_along_axis(U, h[:, m:m + 1], 2) - z), axis=1) for m in range(16)], axis=1)
    m = np.argmin(d, axis=1)[:, None, :]
    return np.take_along_axis(h, m, 1)[:, 0], np.take_along_axis(d, m, 1)[:, 0] < b[:, None]
def lowest(h, fit):
    win = np.zeros(fit.shape, bool)
    for g in range(8):
        i = np.flatnonzero(fit[g]); win[g, i[np.unique(h[g, i], return_index=True)[1]]] = True
    return win
def parts(rng):
    return (rng.integers(0, 256, (N, 8, 16, S), dtype=np.int16), rng.integers(0, 256, (N, 8, 16, S), dtype=np.int16), rng.integers(0, S, (N, 8, L)),
            rng.integers(0, 4096, (N, 8, 16, 2)), rng.integers(0, KM + 1, (N, 8, 16)), rng.integers(840, 1040, (N, 8)))
def pack(us, tp, c, w, k, th):
    return {"us": us.reshape(N, 128, S).astype(np.float32).astype(BF), "tp": tp.reshape(N, 128, S).astype(np.float32).astype(BF), "c0": np.ascontiguousarray(c).astype(np.int32),
            "hw": np.ascontiguousarray(w.reshape(N, 128, 2)).astype(np.int32), "km": np.ascontiguousarray(k.reshape(N, 128, 1)).astype(np.int32), "th": np.ascontiguousarray(th.reshape(N, 8, 1)).astype(np.int32)}
def setup_inputs(rng):
    return pack(*parts(rng))
def near(z, d):
    a = d[None, :] // 16 + (np.arange(16)[:, None] < d[None, :] % 16)
    return np.where(z < 128, z + a, z - a)
def setup_inputs_corners(rng):
    us, tp, c, w, k, th = parts(rng); w[:, :, 0, 0] |= 1; cnt = (0, 1, CAP - 1, CAP, CAP + 1, L); used = {}; sent = {}; zs = []
    def plant(q, g, h, z, todo):
        st, sl, ds = [], [], []
        for i, d in todo:
            r = int(rng.integers(0, 16)); cand = h[:, i].tolist()
            for m in range(16):
                s = cand[(m + r) % 16]
                if s not in used[q, g]:
                    used[q, g].add(s); st.append(s); sl.append(i); ds.append(d); break
        if st: us[q, g][:, np.array(st)] = near(z[:, np.array(sl)], np.array(ds))
    for q in range(N):
        for g in range(8):
            v = (g + q) % 8; used[q, g] = set()
            if v == 6: c[q, g] = 4 * rng.integers(0, S // 4, L) + 3; c[q, g, :3] = S - 1
            elif v == 7: c[q, g] = 4 * rng.integers(0, S // 4, L); c[q, g, L - 3:] = 0
            else: c[q, g] = 4 * rng.permutation(S // 4)[:L] + 1; k[q, g] = rng.permutation(min(S, KM + 1))[:16]; th[q, g] = rng.choice(np.array([1, 2, 64, 100]))
            if v in (1, 2, 3): us[q, g, :, 0] = 0; used[q, g].add(0)
        p, z = joined(c[q], tp[q]); even = (np.sum(z * w[q, :, :, 0:1], axis=1) & 1) == 0
        for g in range(8):
            if (g + q) % 8 < 6: tp[q, g, 8, np.unique(p[g, even[g]])] ^= 1
        p, z = joined(c[q], tp[q]); zs.append(z); h = places(z, w[q], k[q])
        for g in range(8):
            v = (g + q) % 8
            if v > 5: continue
            n = cnt[v]; pair = 2 if n >= 2 else 0; front = rng.permutation(L - 2).tolist(); t = int(th[q, g])
            poor = front[:n - pair] + ([L - 2, L - 1] if pair else []); fits = front[n - pair:] + ([] if pair else [L - 2])
            plant(q, g, h[g], z[g], [(i, (t - 1) * int(rng.integers(0, 2))) for i in fits] + [(i, t) for i in poor if i < L - 1 and rng.random() < 0.5])
            sent[q, g] = sorted(poor)[:CAP]
    for q in range(N):
        a = (q + 1) % N; h = places(zs[q], w[a], k[a])
        for g in range(8):
            if (q, g) in sent:
                t = int(th[a, g]); full = (g + q) % 8 == 4
                plant(a, g, h[g], zs[q][g], [(i, (0, t - 1, t)[int(rng.integers(0, 2 if full else 3))]) for i in sent[q, g] if i < L - 1 and (full or rng.random() < 0.6)])
    return pack(us, tp, c, w, k, th)
def setup_inputs_ends(rng):
    us = 255 * rng.integers(0, 2, (N, 8, 16, S), dtype=np.int16); tp = 255 * rng.integers(0, 2, (N, 8, 16, S), dtype=np.int16)
    inner = np.argsort(rng.random((N, 8, L)), axis=-1) < 5 * L // 16; anyc = rng.integers(0, S, (N, 8, L)); roll = rng.random((N, 8, L))
    w = 4095 * rng.integers(0, 2, (N, 8, 16, 2)); w[:, :, 0, 0] = 0; w[:, :, 1, 0] = 4095
    k = np.where(np.argsort(rng.random((N, 8, 16)), axis=-1) < 4, rng.integers(0, KM + 1, (N, 8, 16)), KM * rng.integers(0, 2, (N, 8, 16)))
    th = np.stack([4080 * (rng.permutation(8) % 2) for q in range(N)]); big = np.stack([rng.permutation(8) < 4 for q in range(N)]); big[:, 7] = True; big[0, 0] = True
    if th[N - 1, 7] == 0: th[N - 1, int(np.argmax(th[N - 1]))] = 0; th[N - 1, 7] = 4080
    c = np.where(inner, anyc, (S - 1) * (roll < 0.5)); base = ((S - 1) ** 2 >> 5) & (S - 1); one = np.zeros(16, np.int16); one[0] = 1
    for q in range(N):
        for g in range(8):
            if not big[q, g]: continue
            w[q, g] = 4095; us[q, g, :, 0] = 255; tp[q, g, :, 0] = 255; tp[q, g, :, S - 1] = 0; tp[q, g, :, S - 2] = 0; tp[q, g, 8, S - 2] = 1
            far = (S - 1, 1, 2) if g == 7 or rng.random() < 0.5 else (2, S - 1, 1)
            for lane, s in zip((1, 14, 15), far): k[q, g, lane] = (base - s) & (S - 1); us[q, g, :, s] = one
            k[q, g, 0] = 0; k[q, g, 2] = KM
            c[q, g] = np.where(inner[q, g], anyc[q, g] // 4 * 4, (S - 1) * (roll[q, g] < 0.2))
            if rng.random() < 0.5: c[q, g, 0] = S - 2; c[q, g, 1] = S - 1
            c[q, g, 4:6] = S - 1; c[q, g, 6:9] = 0; c[q, g, L - 2] = S - 2; c[q, g, L - 1] = S - 1
    return pack(us, tp, c, w, k, th)
def setup_inputs_refuse(rng):
    d = setup_inputs_ends(rng); d["th"][1] = 0
    return d
def setup_inputs_spread(rng):
    us, tp, c, w, k, th = parts(rng)
    def stones():
        v = np.floor(np.exp2(8 * rng.random((N, 8, 1, S), dtype=np.float32)) * rng.random((N, 8, 16, S), dtype=np.float32)).astype(np.int16)
        v = np.minimum(v, 255); return np.where(rng.random((N, 8, 1, S)) < 0.25, 255 - v, v)
    c = np.minimum((S * rng.random((N, 8, L)) ** 3).astype(np.int64), S - 1); c[:, ::2] = S - 1 - c[:, ::2]
    w = np.minimum(np.exp2(12.01 * rng.random((N, 8, 16, 2))).astype(np.int64) - (rng.random((N, 8, 16, 2)) < 0.05), 4095)
    k = np.maximum(np.minimum(np.exp2(12 * rng.random((N, 8, 16))).astype(np.int64) - 1, KM), 0)
    th = np.where(rng.random((N, 8)) < 0.25, rng.integers(0, 4081, (N, 8)), np.exp2(6 + 4 * rng.random((N, 8))).astype(np.int64))
    us = stones(); tp = stones()
    for q in range(N):
        g = int(rng.integers(0, 8))
        us[q, g] = rng.integers(0, 8, (16, S)); us[q, g, 0] += 248
        tp[q, g] = rng.integers(248, 256, (16, S)); tp[q, g, 8] = rng.integers(0, 2, S)
        w[q, g, :, 0] = 3072; w[q, g, 0, 0] = 4095; w[q, g, :, 1] = rng.integers(0, 4096, 16)
        k[q, g] = rng.permutation(KM + 1)[:16]; th[q, g] = 4080
    return pack(us, tp, c, w, k, th)
def setup_inputs_ties(rng):
    us, tp, c, w, k, th = parts(rng); flat = int(rng.integers(0, 8)); z = np.full((1, 16, 1), 255); z[0, 0] = 0
    for q in range(N):
        for g in range(8):
            pr = rng.integers(0, 256, (16, 12)); tp[q, g] = pr[:, rng.integers(0, 12, S)]
            us[q, g, :8] = pr[8:, rng.integers(0, 12, S)]; us[q, g, 8:] = pr[:8, rng.integers(0, 12, S)]
            th[q, g] = int(rng.choice(np.array([1, 400, 600, 700, 900])))
        us[q, flat] = 0; us[q, flat, 0] = 255; tp[q, flat] = 255; tp[q, flat, 8] = 0; th[q, flat] = 4080
        w[q, flat, 1, 0] ^= 1 - int(np.sum(w[q, flat, 1:, 0])) % 2
        if places(z, w[q, flat][None], k[q, flat][None])[0, 0, 0] == 0: k[q, flat, 0] ^= 1
    return pack(us, tp, c, w, k, th)
def check_inputs(d):
    bad = []
    for a, lo, hi in (("us", 0, 255), ("tp", 0, 255), ("c0", 0, S - 1), ("hw", 0, 4095), ("km", 0, KM), ("th", 0, 4080)):
        v = np.asarray(d[a]).astype(np.float64)
        if not (np.min(v) >= lo and np.max(v) <= hi): bad.append("range of " + a)
        elif np.any(v != np.floor(v)): bad.append("whole numbers in " + a)
    return bad
def reference(us, tp, c0, hw, km, th):
    U = np.zeros((N, 8, 16, W), np.int64); U[..., :S] = us.astype(np.float32).astype(np.int64).reshape(N, 8, 16, S)
    T = np.zeros((N, 8, 16, W), np.int64); T[..., :S] = tp.astype(np.float32).astype(np.int64).reshape(N, 8, 16, S)
    C = c0.astype(np.int64); w = hw.astype(np.int64).reshape(N, 8, 16, 2); k = km.astype(np.int64).reshape(N, 8, 16); t0 = th.astype(np.int64).reshape(N, 8)
    P = np.zeros(N, np.int64); out = []
    for t in range(RO):
        b = t0 + (P & 63)[:, None]; new, poor, zs = [], [], []
        for a in range(N):
            p, z = joined(C[a], T[a]); h, fit = probe(z, w[a], k[a], b[a], U[a]); win = lowest(h, fit)
            for g in range(8): U[a, g][:, h[g, win[g]]] = 255
            new.append(np.where(win, h, p)); poor.append(~fit); zs.append(z)
        for q in range(N):
            a = (q + 1 + t % (N - 1)) % N; sl = [np.flatnonzero(poor[q][g])[:CAP] for g in range(8)]
            z = np.zeros((8, 16, CAP), np.int64); use = np.zeros((8, CAP), bool)
            for g in range(8): z[g][:, :len(sl[g])] = zs[q][g][:, sl[g]]; use[g, :len(sl[g])] = True
            h, fit = probe(z, w[a], k[a], b[a], U[a]); win = lowest(h, fit & use)
            for g in range(8):
                s = np.flatnonzero(win[g]); n = h[g, s]; own = S + CAP * t + s
                U[q, g][:, own] = U[a, g][:, n]; T[q, g][:, own] = T[a, g][:, n]; U[a, g][:, n] = 255; new[q][g, sl[g][s]] = own
        P = np.array([int(np.sum(m)) for m in poor]); C = np.stack(new); out.append(C)
    return {"yc": np.concatenate(out, axis=2).astype(np.float32), "yu": U.reshape(N, 128, W).astype(np.float32).astype(BF)}

@@ -1,0 +1,673 @@
+from concourse.mybir import AluOpType, AxisListType, ActivationFunctionType
+
+NB, NA, S, W, R = 32, 6, 4096, 4384, 3
+ZC, UW = 4608, 4624
+SG = (1, 9)
+F, B, I, H, U16 = "float32", "bfloat16", "int32", "float16", "uint16"
+SCRATCH, PACK, PACKED = {}, {}, {}
+SEMAPHORES = ["sv", "ss", "sp", "sg", "d0", "d1", "d2", "d3", "d4", "d5", "dt", "lz", "ly", "lx"] + ["du%d" % t for t in range(4)]
+for _t in range(R):
+    SEMAPHORES += ["az%d" % _t, "ar%d" % _t, "au%d" % _t]
+    SCRATCH["ZR%d" % _t] = ("sbuf", [128, 96], B)
+    SCRATCH["RB%d" % _t] = ("sbuf", [128, 192], B)
+for _n in range(8):
+    SCRATCH["p%d" % _n] = ("psum", [128, 512], F)
+for _w, _d, _s in (
+        (UW, B, "U Tw FL"), (288, B, "UP"), (32, I, "CR"), (2048, B, "E2 E3 FX FD EH EL E1 LQ"), (2048, H, "WU WV KD"), (16384, B, "EQ"),
+        (512, F, "KD2 ior DA DB KA KB YC"), (2, I, "pi pq hwi"), (1, I, "kmi thi Pi Pj"), (1, F, "pf qf gf kmf thf"), (2, F, "hwf hwg hws hwm"),
+        (16, F, "io16 qm ql kq KM KS0 KS dA dB dC"), (16, I, "ki ka kb"), (128, F, "io8 io128 iox BF x1 x2 x3 x4 x5 x6 rep"), (128, B, "BD ID NI GE BH BL ZM"), (128, F, "O16"),
+        (96, F, "msk CA CB Hd"), (32, F, "col tc tcq tc512 tc1024 tc4096 W40 W4 on idx T1 nf pen0 pen cum s1 OF lf hx hx0 wl ld hm lo l2 Cf cw ee ec mu rc pj pj2 fo jt jj a1 a2 a3 a4 a5 a6 a7 n1 n2 n3 n4 n5"),
+        (32, I, "PR qi kk ks k2 k3 Hh Ci f3 fi nx Ai"), (64, I, "uva uv kI kJ dg"), (32, H, "uh qh hh"), (6, H, "ha"), (64, B, "dh dn"), (32, B, "pw wv"),
+        (32, U16, "OFu lou fou JJ JB ngu"), (8, U16, "glu sou"), (64, U16, "CL"), (512, U16, "HL HR"), (512, I, "X X2"),
+        (512, B, "JV L255 NB2 NG ZA Z TC GS LS JS DF0 DF1 DF2"), (1024, B, "JP NW JW AB0 AB1 AB2"), (528, B, "NR"), (1536, B, "ZS TS"), (384, B, "z4"), (576, F, "EA"),
+        (8, F, "la rA rB k6 k7 gt gl gm gm0 gn go gp gh"), (48, F, "t48 v48"), (24, F, "t24 v24"), (12, F, "t12 v12"), (192, B, "SB"), (96, B, "SU xt")):
+    for _n in _s.split():
+        if _w <= 64 and _n not in ("CR", "hwi", "kmi", "thi"):
+            _k = "pk" + _d
+            PACK[_n] = (_k, PACKED.get(_k, 0), _w)
+            PACKED[_k] = PACKED.get(_k, 0) + (_w + 7) // 8 * 8
+        else:
+            SCRATCH[_n] = ("sbuf", [128, _w], _d)
+for _k, _w in PACKED.items():
+    SCRATCH[_k] = ("sbuf", [128, _w], _k[2:])
+
+
+def rank_program(g, core, T, topo):
+    rank = T.rank_of(core)
+    if rank is None:
+        return
+    A, AF, X = AluOpType, ActivationFunctionType, AxisListType.X
+    Q = {"V": g.vector, "S": g.scalar, "P": g.tensor, "G": g, "Y": g.sync}
+    SEM = {"V": "sv", "S": "ss", "P": "sp", "G": "sg"}
+    count, known, snaps, rec = {}, {q: {} for q in Q}, {}, {}
+
+    def v(name, lo=None, hi=None, step=1, p=None):
+        buf, at, w = PACK[name] if name in PACK else (name, 0, SCRATCH[name][1][1])
+        lo = 0 if lo is None else lo
+        hi = w if hi is None else hi
+        rows = slice(None) if p is None else p
+        ap = T[buf][rows, at + lo:at + hi] if step == 1 else T[buf][rows, at + lo:at + hi:step]
+        return (ap, name, lo, hi, step)
+
+    def ind(win, off):
+        return (win[0].indirect(off[0]), (win, off))
+
+    def parts(x):
+        return list(x[1]) if len(x) == 2 else [x]
+
+    def hit(a, b):
+        if a[1] >= b[2] or b[1] >= a[2]:
+            return False
+        return not (a[3] == b[3] and a[3] > 1 and (a[1] - b[1]) % a[3])
+
+    def is_bank(n):
+        return n[0] == "p" and n[1:].isdigit()
+
+    def reg(x):
+        return (x[1], 0, 512, 1) if is_bank(x[1]) else (x[1], x[2], x[3], x[4])
+
+    def learn(q, e, n):
+        known[q][e] = max(known[q].get(e, 0), n)
+        for e2, n2 in snaps.get((e, n), {}).items():
+            known[q][e2] = max(known[q].get(e2, 0), n2)
+
+    def settle(q, reads, writes):
+        need = {}
+        for xs, isw in ((reads, False), (writes, True)):
+            for x in xs:
+                r = reg(x)
+                ps = is_bank(r[0])
+                for (o, e, n, w) in rec.get(r[0], []):
+                    if not hit(r, o):
+                        continue
+                    if e == q:
+                        if q == "P" or not (w or isw):
+                            continue
+                    elif not (w or isw or ps):
+                        continue
+                    need[e] = max(need.get(e, 0), count[e] if e[0] in "DL" else n)
+        for e, n in sorted(need.items(), key=lambda kv: -kv[1]):
+            if known[q].get(e, 0) < n:
+                Q[q].wait_ge(T.sem[SEM.get(e, e[1:])], n)
+                learn(q, e, n)
+
+    def note(e, n, reads, writes, snap):
+        snaps[(e, n)] = dict(snap)
+        for xs, isw in ((reads, False), (writes, True)):
+            for x in xs:
+                r = reg(x)
+                old = rec.setdefault(r[0], [])
+                if isw:
+                    old[:] = [o for o in old if not (o[0][1] >= r[1] and o[0][2] <= r[2] and r[3] == 1)]
+                old[:] = [o for o in old if not (o[0] == r and o[1] == e and o[3] == isw)]
+                old.append((r, e, n, isw))
+
+    def op(q, f, reads, writes):
+        rs = [p for x in reads if isinstance(x, tuple) for p in parts(x)]
+        ws = []
+        for x in writes:
+            ps = parts(x)
+            ws.append(ps[0])
+            rs += ps[1:]
+        settle(q, rs, ws)
+        count[q] = count.get(q, 0) + 1
+        f().then_inc(T.sem[SEM[q]], 1)
+        note(q, count[q], rs, ws, known[q])
+
+    def dma(q, sem, out, in_, reads, writes):
+        settle(q, reads, writes)
+        e = "D" + sem
+        count[e] = count.get(e, 0) + 16
+        Q[q].dma_start(out, in_).then_inc(T.sem[sem], 16)
+        note(e, count[e], reads, writes, known[q])
+
+    def _(x):
+        return x[0] if isinstance(x, tuple) else x
+
+    def ts(o, i, s1, op0, s2=None, op1=None):
+        rd = [i, s1, s2]
+        if op1 is None:
+            op("V", lambda: g.vector.tensor_scalar(out=_(o), in0=_(i), scalar1=_(s1), scalar2=None, op0=op0), rd, [o])
+        else:
+            op("V", lambda: g.vector.tensor_scalar(out=_(o), in0=_(i), scalar1=_(s1), scalar2=_(s2), op0=op0, op1=op1), rd, [o])
+
+    def tt(o, a, b, op0):
+        op("V", lambda: g.vector.tensor_tensor(out=_(o), in0=_(a), in1=_(b), op=op0), [a, b], [o])
+
+    def cp(o, i):
+        op("V", lambda: g.vector.tensor_copy(out=_(o), in_=_(i)), [i], [o])
+
+    def ms(o, c):
+        op("V", lambda: g.vector.memset(_(o), c), [], [o])
+
+    def scan(o, a, b, init, op0, op1):
+        op("V", lambda: g.vector.tensor_tensor_scan(_(o), _(a), _(b), init, op0, op1), [a, b], [o])
+
+    def act(o, i, func=AF.Copy, scale=None, bias=None):
+        kw = {}
+        if scale is not None:
+            kw["scale"] = _(scale)
+        if bias is not None:
+            kw["bias"] = _(bias)
+        op("S", lambda: g.scalar.activation(_(o), _(i), func, **kw), [i, scale, bias], [o])
+
+    def mm(o, l, r, start=True, stop=True):
+        op("P", lambda: g.tensor.matmul(_(o), _(l), _(r), start, stop), [l, r], [o])
+
+    def iota(o, pattern, base, cm, flag=True):
+        op("G", lambda: g.iota(_(o), pattern, base, cm, allow_small_or_imprecise_dtypes=True) if flag else g.iota(_(o), pattern, base, cm), [], [o])
+
+    def col(j):
+        return v("col", j, j + 1)
+
+    def mat(name, q):
+        return v(name, 128 * q, 128 * q + 128)
+
+    def send(sem, lsem, dst, out, in_, reads):
+        settle("G", reads, [])
+        es = topo.engines(core, dst)[:8]
+        rid, pid, se = topo.addr(dst)
+        e = "L" + lsem
+        count[e] = count.get(e, 0) + len(es)
+        g.remote_dma(out, in_, T.sem[sem], T.sem[lsem], pid, rid, sum(1 << k for k in es))
+        note(e, count[e], reads, [], known["G"])
+
+    for t in range(R):
+        asker, lender = T.cores[(rank - 1 - t) % 8], T.cores[(rank + 1 + t) % 8]
+        for sem, src, ws in (("az%d" % t, asker, [v("ZR%d" % t)]), ("ar%d" % t, lender, [v("RB%d" % t)]), ("au%d" % t, lender, [v("UP", 96 * t, 96 * t + 96)])):
+            n = len(topo.engines(src, core)[:8])
+            count["A" + sem] = n
+            note("A" + sem, n, [], ws, {})
+
+    dma("Y", "d0", T.CR[:, :], T.c0[:, :], [], [v("CR")])
+    dma("S", "d1", T.hwi[:, :], T.hw[:, :], [], [v("hwi")])
+    dma("S", "d1", T.kmi[:, :], T.km[:, :], [], [v("kmi")])
+    for k in range(16):
+        lo = 8 * k
+        dma("S" if k % 2 else "Y", "d2", T.Tw[lo:lo + 8, 0:S], T.tp[(lo ^ 8):(lo ^ 8) + 8, :], [], [v("Tw", 0, S)] if k == 15 else [])
+    dma("Y", "dt", T.thi[0:8, :], T.th[:, :], [], [v("thi")])
+    for k in range(4):
+        dma("Y", "du%d" % k, T.U[:, 1024 * k:1024 * k + 1024], T.us[:, 1024 * k:1024 * k + 1024], [], [v("U", 1024 * k, 1024 * k + 1024)])
+
+    iota(v("pi"), [[0, 2]], 0, 1, False)
+    iota(v("io16"), [[1, 16]], 0, 0)
+    iota(v("io8"), [[1, 8], [0, 16]], 0, 0)
+    iota(v("iox"), [[0, 8], [1, 16]], 0, 0)
+    iota(v("io128"), [[1, 128]], 0, 0)
+    iota(v("E2"), [[-1, 16], [32, 8], [1, 16]], 0, 0)
+    iota(v("E3"), [[1, 16], [32, 8], [0, 16]], 0, 0)
+    iota(v("tc"), [[16, 32]], 0, 0)
+    iota(v("ior"), [[1, 512]], -256, 0)
+    iota(v("FL", 0, ZC), [[0, ZC]], 0, 0)
+    iota(v("FL", ZC, UW), [[0, UW - ZC]], 1, 0)
+    cp(v("pf"), v("pi", 0, 1))
+    ts(v("pq", 0, 1), v("pi", 0, 1), 4, A.arith_shift_right)
+    ts(v("pq", 1, 2), v("pi", 0, 1), 15, A.bitwise_and)
+    cp(v("gf"), v("pq", 0, 1))
+    cp(v("qf"), v("pq", 1, 2))
+    ts(v("qm"), v("io16"), v("qf"), A.is_equal)
+    ts(v("BD"), v("io8"), v("gf"), A.is_equal)
+    ts(v("x1"), v("iox"), 2.0, A.is_equal, 128.0, A.mult)
+    ts(v("x2"), v("iox"), 0.0, A.is_equal)
+    tt(v("x3"), v("x1"), v("x2"), A.add)
+    tt(v("BH"), v("x3"), v("BD"), A.mult)
+    for q in range(16):
+        act(mat("EH", q), v("BH"), scale=v("qm", q, q + 1))
+    ts(v("x4"), v("iox"), 2.0, A.is_equal)
+    ts(v("x5"), v("iox"), 1.0, A.is_equal)
+    tt(v("x6"), v("x4"), v("x5"), A.add)
+    tt(v("BL"), v("x6"), v("BD"), A.mult)
+    for q in range(16):
+        ts(mat("EL", q), v("BL"), v("qm", q, q + 1), A.mult)
+    ts(v("dg", 0, 32), v("CR"), 7, A.arith_shift_right)
+    ts(v("dg", 32, 64), v("CR"), 127, A.bitwise_and)
+    cp(v("dh"), v("dg"))
+    for q in range(16):
+        mm(v("p6", 32 * q, 32 * q + 32), mat("EH", q), v("dh", 0, 32), True, False)
+        mm(v("p6", 32 * q, 32 * q + 32), mat("EL", q), v("dh", 32, 64), False, True)
+    ms(v("NR", 512, 528), 0.0)
+    act(v("NR", 0, 512), v("p6"))
+    ts(col(0), v("qf"), 7.5, A.is_lt)
+    ts(col(4), v("qm", 0, 1), 128.0, A.mult)
+    tt(col(15), col(4), v("qm", 1, 2), A.add)
+    ts(col(13), v("gf"), 32.0, A.mult)
+    tt(col(14), col(13), v("qf"), A.add)
+    ts(v("FX"), v("E2"), col(13), A.is_equal, col(15), A.mult)
+    ts(v("BF"), v("io8"), v("gf"), A.is_equal)
+    ts(col(1), col(0), -512.0, A.mult, 256.0, A.add)
+    ts(col(2), col(0), -256.0, A.mult)
+    ts(col(3), col(0), 256.0, A.mult)
+    ts(col(5), col(0), -256.0, A.mult, 255.0, A.add)
+    ts(col(6), v("qm", 1, 2), -512.0, A.mult)
+    for n, lo, hi in (("Tw", S, UW), ("U", S, ZC)):
+        ms(v(n, lo, hi), 0.0)
+    cp(v("hwf"), v("hwi"))
+    ts(v("hwg"), v("hwf"), 2048.0, A.is_ge, -4096.0, A.mult)
+    tt(v("hws"), v("hwg"), v("hwf"), A.add)
+    ts(v("hwm"), v("hws"), col(3), A.mult)
+    cp(v("kmf"), v("kmi"))
+    ts(v("kq"), v("qm"), v("kmf"), A.mult)
+    mm(v("p5", 0, 2), v("BF"), v("hwm"))
+    mm(v("p5", 2, 18), v("BF"), v("kq"))
+    ts(v("WU"), v("E2"), col(13), A.is_equal, v("hws", 0, 1), A.mult)
+    cp(v("col", 7, 9), v("p5", 0, 2))
+    cp(v("KM"), v("p5", 2, 18))
+    ts(v("WV"), v("E2"), col(13), A.is_equal, v("hws", 1, 2), A.mult)
+    ts(v("ID"), v("io128"), v("pf"), A.is_equal)
+    ts(v("KS0"), v("KM"), 2048.0, A.is_ge, -4096.0, A.mult)
+    tt(v("KS"), v("KS0"), v("KM"), A.add)
+    ts(v("U", ZC, UW), v("Tw", ZC, UW), col(2), A.add)
+
+    def setup_hash():
+        for m in range(16):
+            ts(mat("KD", m), v("ID"), v("KS", m, m + 1), A.mult)
+        ts(v("NI"), v("ID"), -1.0, A.mult)
+
+    def setup_fill():
+        act(v("NW", 512, 1024), v("p6"))
+        act(v("JV"), v("ior"), scale=v("qm", 1, 2))
+        act(v("JP"), v("E2", 0, 1024), AF.Identity, scale=0.0, bias=col(6))
+        act(v("JW"), v("JP"))
+        act(v("L255"), v("E2", 0, 512), AF.Identity, scale=0.0, bias=col(5))
+
+    def setup_late():
+        ts(v("FD"), v("E2"), col(13), A.is_equal, 4096.0, A.mult)
+        cp(v("ki"), v("KM"))
+        ts(v("ka"), v("ki"), 4, A.arith_shift_right)
+        ts(v("kb"), v("ki"), 15, A.bitwise_and)
+        ts(v("dC"), v("io16"), 256.0, A.mult)
+        tt(v("dB"), v("dC"), v("kb"), A.add)
+        tt(v("dA"), v("dC"), v("ka"), A.add)
+
+    def setup_last():
+        yield
+        for d, D, C in (("dA", "DA", "CA"), ("dB", "DB", "CB")):
+            tt(v(D, 1, 16), v(d, 0, 15), v(d, 1, 16), A.subtract)
+            ms(v(D, 0, 1), 33554432.0)
+            w = 16
+            while w < 512:
+                act(v(D, w, 2 * w), v(D, 0, w))
+                w *= 2
+            for b in range(NA):
+                cp(v(C, b, 96, NA), v(d))
+        yield
+        ts(v("rep", p=slice(0, 8)), v("io8", p=slice(0, 8)), v("pf", p=slice(0, 8)), A.is_equal)
+        cp(v("thf", p=slice(0, 8)), v("thi", p=slice(0, 8)))
+        mm(v("p5", 0, 1), v("rep", p=slice(0, 8)), v("thf", p=slice(0, 8)))
+        ts(v("x1"), v("io128"), v("pf"), A.is_le)
+        tt(v("GE"), v("x1"), v("BD"), A.mult)
+        ms(v("on"), 1.0)
+        ts(v("tcq"), v("tc"), v("qf"), A.add)
+        yield
+        for n in (512, 1024, 4096):
+            ts(v("tc%d" % n), v("tcq"), float(n), A.add)
+        ts(v("W40"), v("tcq"), 510.0, A.is_equal, 5112.0, A.mult)
+        ts(v("W4"), v("W40"), 4.0, A.add)
+        cp(col(9), v("p5", 0, 1))
+        ts(col(10), col(9), 4081.0, A.min, 4096.0, A.mult)
+        tt(col(11), col(10), v("dA", 15, 16), A.subtract)
+        yield
+        ms(v("O16"), 0.0625)
+        ms(v("ZM"), 0.0)
+        ts(v("ql"), v("io16"), v("qf"), A.is_gt)
+        for q in range(1, 16):
+            act(mat("LQ", q), v("BD"), scale=v("ql", q, q + 1))
+        ms(v("ZS", 0, 96), 1024.0)
+        ms(v("TS", 0, 96), 0.0)
+        yield
+        ts(v("E1"), v("E3"), col(14), A.is_equal)
+        ts(v("msk"), v("iox", 0, 96), v("qf"), A.is_ge, 30000.0, A.mult)
+        yield
+
+    def to_list(ps, row, lo=0, n=512):
+        for q in range(16):
+            mm(ps, mat("FX", q), v(row, lo + q, lo + n, 16), q == 0, q == 15)
+
+    def digits(src, name="dh"):
+        ts(v("dg", 0, 32), src, 7, A.arith_shift_right)
+        ts(v("dg", 32, 64), src, 127, A.bitwise_and)
+        cp(v(name), v("dg"))
+
+    def rows(name):
+        for q in range(16):
+            mm(v("p6", q, 512, 16), mat("EH", q), v(name, 0, 32), True, False)
+            mm(v("p6", q, 512, 16), mat("EL", q), v(name, 32, 64), False, True)
+
+    def hash_sums(z, nb):
+        n = 16 * nb
+        for j, w in ((0, "WU"), (1, "WV")):
+            for q in range(16):
+                mm(v("p0", 32 * j, 32 * j + nb), mat(w, q), v(z, q, n, 16), q == 0, q == 15)
+
+    def hash_uv(nb):
+        ts(v("uva", 0, nb), v("p0", 0, nb), col(7), A.add)
+        ts(v("uva", nb, 2 * nb), v("p0", 32, 32 + nb), col(8), A.add)
+        ts(v("uv", 0, 2 * nb), v("uva", 0, 2 * nb), 4095, A.bitwise_and)
+        tt(v("PR", 0, nb), v("uv", 0, nb), v("uv", nb, 2 * nb), A.mult)
+        ts(v("T1", 0, nb), v("uv", 0, nb), 2048.0, A.is_ge, -4096.0, A.mult)
+        ts(v("qi", 0, nb), v("PR", 0, nb), 5, A.arith_shift_right, 4095, A.bitwise_and)
+        tt(v("uh", 0, nb), v("T1", 0, nb), v("uv", 0, nb), A.add)
+        ts(v("qh", 0, nb), v("qi", 0, nb), -2048.0, A.add)
+
+    def hash_lists(nb, half):
+        ps = "p3" if half else "p1"
+        for m in range(8 * half, 8 * half + 8):
+            o = v(ps, (m - 8 * half) * nb, (m - 8 * half) * nb + nb)
+            mm(o, mat("KD", m), v("uh", 0, nb), True, False)
+            mm(o, v("ID"), v("qh", 0, nb), False, True)
+
+    def lists(half, nb):
+        w, o = 8 * nb, 8 * nb * half
+        ts(v("X", o, o + w), v("p3" if half else "p1", 0, w), 2048.0, A.add)
+        ts(v("X2", o, o + w), v("X", o, o + w), 4095, A.bitwise_and)
+        cp(v("HL", o, o + w), v("X2", o, o + w))
+
+    def best(nb, ka, da, kb, db):
+        ts(v("kI", 0, nb), ka, da, A.add)
+        ts(v("kI", nb, 2 * nb), kb, db, A.add)
+        ts(v("kJ", 0, 2 * nb), v("kI", 0, 2 * nb), 255, A.bitwise_and)
+        ts(v("kk", 0, nb), v("kJ", 0, nb), 16.0, A.mult)
+        tt(v("ks", 0, nb), v("kk", 0, nb), v("kJ", nb, 2 * nb), A.add)
+        tt(v("k2", 0, nb), v("ks", 0, nb), v("uv", 0, nb), A.mult)
+        tt(v("k3", 0, nb), v("k2", 0, nb), v("qi", 0, nb), A.add)
+        ts(v("Hh", 0, nb), v("k3", 0, nb), 4095, A.bitwise_and)
+
+    def widths():
+        ts(v("f3"), v("Ci"), 3, A.bitwise_and)
+        tt(v("wv"), v("f3"), v("W4"), A.add)
+        mm(v("p5", 64, 96), v("BD"), v("wv"))
+        mm(v("p5", 96, 128), v("GE"), v("wv"))
+        yield
+        yield
+        scan(v("cw"), v("on"), v("p5", 64, 96), 0.0, A.mult, A.add)
+        tt(v("ee"), v("cw"), v("p5", 96, 128), A.subtract)
+        tt(v("ec"), v("ee"), v("wv"), A.add)
+        yield
+        ts(v("fi"), v("ee"), 0.2, A.mult, 512.0, A.min)
+        ts(v("nx"), v("ec"), 0.2, A.mult, 512.0, A.min)
+        tt(v("mu"), v("nx"), v("fi"), A.subtract)
+        yield
+        ts(v("rc"), v("mu"), 0.5, A.is_ge)
+        ts(v("pj"), v("mu"), 0.5, A.is_lt)
+        tt(v("pj2"), v("pj"), v("tc512"), A.mult)
+        tt(v("fo"), v("fi"), v("pj2"), A.max)
+        cp(v("fou"), v("fo"))
+        yield
+
+    def slots():
+        cp(ind(v("JW"), v("fou")), v("JV"))
+        scan(v("JS"), v("JW", 0, 512), v("JW", 0, 512), -512.0, A.max, A.max)
+
+    def slots_lists():
+        to_list(v("p4", 0, 32), "JS")
+        to_list(v("p4", 32, 64), "JW")
+
+    def slots2():
+        ts(v("jt"), v("p4", 32, 64), -256.5, A.is_lt, 512.0, A.mult)
+        ts(v("JB"), v("p4", 0, 32), 768.0, A.add)
+        tt(v("jj"), v("jt"), v("p4", 0, 32), A.add)
+        ts(v("JJ"), v("jj"), 256.0, A.add)
+
+    def numbers(t):
+        act(v("NG"), ind(v("RB%d" % t, 96, 192), v("ngu")))
+        yield
+        to_list(v("p4", 96, 128), "NG")
+        yield
+        ts(v("n1"), v("p4", 96, 128), 0.5, A.is_ge)
+        tt(v("n3"), v("n1"), v("n2"), A.mult)
+        tt(v("n5"), v("n3"), v("n4"), A.mult)
+        tt(v("Cf"), v("n5"), v("idx"), A.add)
+        cp(v("Ci"), v("Cf"))
+        digits(v("Ci"), "dn")
+        yield
+        rows("dn")
+        yield
+        if t < R - 1:
+            act(v("NW", 512, 1024), v("p6"))
+        yield
+
+    def put_numbers(t):
+        act(v("YC"), v("p6"))
+        dma("Y", "d3", T.yc[:, 512 * t:512 * t + 512], T.YC[2:128:16, :], [v("YC")], [])
+
+    def u_fix(k, c):
+        x = v("U", 1024 * k, 1024 * k + 1024)
+        if k % 2:
+            ts(x, x, col(c), A.add)
+        else:
+            act(x, x, AF.Identity, bias=col(c))
+        return x
+
+    def next_lists():
+        to_list(v("p0", 0, 32), "NR")
+        to_list(v("p0", 32, 64), "NR", 1)
+
+    def gather(m):
+        act(v("GS"), ind(v("U", 0, S), v("HL", 32 * m, 32 * m + 32)))
+
+    def diff_of(m):
+        o = 512 * (m % 2)
+        return v("AB%d" % (m // 2 % 3), o, o + 512)
+
+    def sum_up(k):
+        bank = "p7" if k % 2 else "p2"
+        for q in range(16):
+            mm(v(bank, 64 * (k // 2), 64 * (k // 2) + 64), mat("FD", q), v("AB%d" % (k % 3), q, 1024, 16), q == 0, q == 15)
+
+    def take(k):
+        bank, o = "p7" if k % 2 else "p2", 64 * (k // 2)
+        for j in (0, 1):
+            act(v("KD2", 2 * k + j, 512, 16), v(bank, o + 32 * j, o + 32 * j + 32))
+
+    def side(t):
+        for x in (numbers(t - 1) if t else setup_last()):
+            yield
+        for x in widths():
+            yield
+
+    next_lists()
+    for t in range(R):
+        last = t == R - 1
+        lender, asker = T.cores[(rank + 1 + t) % 8], T.cores[(rank - 1 - t) % 8]
+        cp(v("CL"), v("p0", 0, 64))
+        if t == 0:
+            cp(v("idx"), v("p0", 0, 32))
+            setup_hash()
+            cp(v("Cf"), v("idx"))
+            cp(v("Ci"), v("idx"))
+            setup_fill()
+        else:
+            tt(v("xt"), v("RB%d" % (t - 1), 96, 192), v("TS", 0, 96), A.mult)
+            tt(v("Tw", S + 96 * t - 96, S + 96 * t), v("xt"), v("RB%d" % (t - 1), 0, 96), A.add)
+        act(v("ZA"), ind(v("Tw", 0, W), v("CL", 0, 32)), AF.Identity, scale=col(0), bias=col(1))
+        todo = side(t)
+        if t:
+            next(todo, None)
+        tt(v("Z"), ind(v("Tw", 0, W), v("CL", 32, 64)), v("ZA"), A.min)
+        if t == 0:
+            for k in range(4):
+                u_fix(k, 2)
+        hash_sums("Z", NB)
+        if t:
+            next(todo, None)
+        hash_uv(NB)
+        hash_lists(NB, 0)
+        hash_lists(NB, 1)
+        if t == 0:
+            setup_late()
+        else:
+            next(todo, None)
+        lists(0, NB)
+        gather(SG[0])
+        ready = []
+        for i, m in enumerate([m for m in range(16) if m not in SG]):
+            df = "DF%d" % (i % 3)
+            tt(v(df), ind(v("U", 0, S), v("HL", 32 * m, 32 * m + 32)), v("Z"), A.subtract)
+            act(diff_of(m), v(df), AF.Abs)
+            for k in ready:
+                take(k)
+            ready = []
+            done = [m // 2] if m % 2 else []
+            if m + 1 in SG:
+                mm(v("p4"), v("ID"), v("GS"), True, False)
+                mm(v("p4"), v("NI"), v("Z"), False, True)
+                act(diff_of(m + 1), v("p4"), AF.Abs)
+                done = [m // 2]
+            if i == 4:
+                lists(1, NB)
+            if i == 5:
+                gather(SG[1])
+            if i >= 1:
+                next(todo, None)
+            for k in done:
+                sum_up(k)
+                ready.append(k)
+        for x in todo:
+            pass
+        for k in ready:
+            take(k)
+        slots()
+        scan(v("KA"), v("DA"), v("KD2"), 0.0, A.add, A.min)
+        ts(v("nf"), v("KA", 15, 512, 16), col(11), A.is_ge)
+        tt(v("pw"), v("nf"), v("mu"), A.mult)
+        mm(v("p5", 0, 32), v("BD"), v("pw"))
+        mm(v("p5", 32, 64), v("GE"), v("pw"))
+        ts(v("pen0"), v("pw"), 0.5, A.is_lt)
+        tt(v("pen"), v("pen0"), v("tc1024"), A.mult)
+        scan(v("cum"), v("on"), v("p5", 0, 32), 0.0, A.mult, A.add)
+        tt(v("s1"), v("cum"), v("p5", 32, 64), A.subtract)
+        tt(v("OF"), v("s1"), v("pen"), A.max)
+        cp(v("OFu"), v("OF"))
+        cp(ind(v("ZS"), v("OFu")), v("Z"))
+        send("az%d" % t, "lz", lender, T["ZR%d" % t][:, :], T.ZS[:, 0:96], [v("ZS", 0, 96)])
+        scan(v("KB"), v("DB"), v("KD2"), 0.0, A.add, A.min)
+        best(NB, v("KA", 15, 512, 16), v("dA", 15, 16), v("KB", 15, 512, 16), v("dB", 15, 16))
+        ts(v("hh"), v("Hh"), -2048.0, A.add)
+        for q in range(16):
+            mm(v("p1", q, 512, 16), mat("E1", q), v("hh"))
+        mm(v("p7"), v("ZM"), v("Z"), True, False)
+        tt(v("lf"), v("rc"), v("nf"), A.is_gt)
+        ts(v("hx0"), v("lf"), -60000.0, A.mult, 60000.0, A.add)
+        tt(v("hx"), v("hx0"), v("Hh"), A.add)
+        tt(v("hm"), v("Hh"), v("tc4096"), A.subtract)
+        tt(v("a1"), v("Hh"), v("Cf"), A.subtract)
+        if not last:
+            act(v("TC"), ind(v("Tw", 0, W), v("CL", 0, 32)))
+        if t:
+            put_numbers(t - 1)
+        ts(v("HR"), v("p1"), 2048.0, A.add)
+        for b in range(NB):
+            e = 512 * b
+            ts(v("EQ", e, e + 512 - 16 * b), v("HR", 16 * b, 512), v("hx", b, b + 1), A.is_equal)
+            if b < NB - 1:
+                mm(v("p7", 16 * b + 16, 512), v("BD"), v("EQ", e + 16, e + 512 - 16 * b), False, False)
+        for q in range(1, 16):
+            mm(v("p7", q, 512, 16), mat("LQ", q), v("EQ", q, 15872 + q + 1, 512), False, q == 15)
+        act(v("LS"), v("p7"))
+        zr = "ZR%d" % t
+        for k in range(4):
+            act(v("z4", 96 * k, 96 * k + 96), v(zr))
+        hash_sums(zr, NA)
+        to_list(v("p5", 192, 224), "LS")
+        if not last:
+            mm(v("p5", 224, 225), v("O16"), v("cum", 31, 32))
+        slots_lists()
+        if not last:
+            cp(ind(v("TS"), v("OFu")), v("TC"))
+        hash_uv(NA)
+        hash_lists(NA, 0)
+        hash_lists(NA, 1)
+        ts(v("wl"), v("p5", 192, 224), 0.5, A.is_lt)
+        tt(v("ld"), v("wl"), v("lf"), A.mult)
+        tt(v("lo"), v("ld"), v("hm"), A.mult)
+        tt(v("l2"), v("lo"), v("tc4096"), A.add)
+        cp(v("lou"), v("l2"))
+        cp(ind(v("U", 0, ZC), v("lou")), v("L255"))
+        if not last:
+            cp(v("Pi"), v("p5", 224, 225))
+        lists(0, NA)
+        lists(1, NA)
+        for k in range(4):
+            df, ab, o = "DF%d" % (k % 3), "AB%d" % (k // 2), 384 * (k % 2)
+            tt(v(df, 0, 384), ind(v("U", 0, S), v("HL", 24 * k, 24 * k + 24)), v("z4"), A.subtract)
+            act(v(ab, o, o + 384), v(df, 0, 384), AF.Abs)
+            if k % 2:
+                for q in range(16):
+                    mm(v("p2", 48 * (k // 2), 48 * (k // 2) + 48), mat("FD", q), v(ab, q, 768, 16), q == 0, q == 15)
+        tt(v("a2"), v("a1"), v("ld"), A.mult)
+        ts(v("a3"), v("OF"), 95.5, A.is_lt)
+        ts(v("a4"), v("OF"), float(S + 96 * t), A.add)
+        tt(v("a5"), v("a4"), v("Cf"), A.subtract)
+        tt(v("a7"), v("a2"), v("Cf"), A.add)
+        tt(v("a6"), v("a5"), v("a3"), A.mult)
+        tt(v("Ai"), v("a7"), v("a6"), A.add)
+        digits(v("Ai"))
+        rows("dh")
+        slots2()
+        act(v("NW", 0, 512), v("p6"))
+        act(v("NR", 0, 512), ind(v("NW"), v("JJ")))
+        tt(v("KA", 0, 96), v("p2", 0, 96), v("CA"), A.add)
+        tt(v("KB", 0, 96), v("p2", 0, 96), v("CB"), A.add)
+        a, b_ = ("KA", 96), ("KB", 96)
+        for na, nb_, w in (("t48", "v48", 48), ("t24", "v24", 24), ("t12", "v12", 12), ("rA", "rB", 6)):
+            tt(v(na, 0, w), v(a[0], 0, w), v(a[0], w, 2 * w), A.min)
+            tt(v(nb_, 0, w), v(b_[0], 0, w), v(b_[0], w, 2 * w), A.min)
+            a, b_ = (na, w), (nb_, w)
+        best(NA, v("rA", 0, NA), 0.0, v("rB", 0, NA), 0.0)
+        ts(v("k6", 0, NA), v("rA", 0, NA), col(10), A.is_ge, 8192.0, A.mult)
+        ts(v("k7", 0, NA), v("Hh", 0, NA), -2048.0, A.add)
+        tt(v("ha"), v("k6", 0, NA), v("k7", 0, NA), A.add)
+        for q in range(16):
+            mm(v("p1", q, 96, 16), mat("E1", q), v("ha"))
+        next_lists()
+        ts(v("gt", 0, NA), v("rA", 0, NA), col(10), A.is_lt)
+        ts(v("gh", 0, NA), v("Hh", 0, NA), float(-ZC), A.add)
+        tt(v("gn", 0, NA), v("Hh", 0, NA), v("tc4096", 0, NA), A.subtract)
+        tt(v("Hd"), v("p1", 0, 96), v("msk"), A.add)
+        for b in range(NA):
+            if b:
+                ts(v("EA", 96 * b, 96 * b + 16 * b), v("p1", 0, 16 * b), v("k7", b, b + 1), A.is_equal)
+            ts(v("EA", 112 * b, 112 * b + 16), v("Hd", 16 * b, 16 * b + 16), v("k7", b, b + 1), A.is_equal)
+        for b in range(NA):
+            o, x = v("la", b, b + 1), v("EA", 96 * b, 112 * b + 16)
+            op("V", lambda: g.vector.tensor_reduce(_(o), _(x), X, A.add), [x], [o])
+        ts(v("gm0", 0, NA), v("la", 0, NA), 0.5, A.is_lt)
+        tt(v("gm", 0, NA), v("gm0", 0, NA), v("gt", 0, NA), A.mult)
+        tt(v("gl", 0, NA), v("gm", 0, NA), v("gh", 0, NA), A.mult)
+        ts(v("glu", 0, NA), v("gl", 0, NA), float(ZC), A.add)
+        act(v("SB", 96, 192), ind(v("FL"), v("glu", 0, NA)))
+        cp(v("SB", 0, 96), ind(v("Tw"), v("glu", 0, NA)))
+        send("ar%d" % t, "ly", asker, T["RB%d" % t][:, :], T.SB[:, :], [v("SB")])
+        act(v("SU"), ind(v("U"), v("glu", 0, NA)))
+        send("au%d" % t, "lx", asker, T.UP[:, 96 * t:96 * t + 96], T.SU[:, :], [v("SU")])
+        act(v("NB2"), ind(v("NW"), v("JB")))
+        if not last:
+            act(v("JW"), v("JP"))
+        to_list(v("p4", 64, 96), "NB2")
+        tt(v("go", 0, NA), v("gn", 0, NA), v("gm", 0, NA), A.mult)
+        tt(v("gp", 0, NA), v("go", 0, NA), v("tc4096", 0, NA), A.add)
+        cp(v("sou", 0, NA), v("gp", 0, NA))
+        cp(ind(v("U", 0, ZC), v("sou", 0, NA)), v("L255", 0, 96))
+        if not last:
+            ts(v("Pj"), v("Pi"), 63, A.bitwise_and)
+            tt(col(16), col(9), v("Pj"), A.add)
+            ts(col(10), col(16), 4081.0, A.min, 4096.0, A.mult)
+            tt(col(11), col(10), v("dA", 15, 16), A.subtract)
+            ms(v("ZS", 0, 96), 1024.0)
+        base = float(S + 96 * t)
+        cp(v("idx"), v("p0", 0, 32))
+        ts(v("ngu"), v("idx"), -base, A.add, 0.0, A.max)
+        ts(v("n2"), v("idx"), base, A.is_ge)
+        if last:
+            for k in range(4):
+                x = u_fix(k, 3)
+                dma("Y", "d4", T.yu[:, 1024 * k:1024 * k + 1024], x[0], [x], [])
+        tt(v("n4"), v("p4", 64, 96), v("idx"), A.subtract)
+
+    for x in numbers(R - 1):
+        pass
+    put_numbers(R - 1)
+    ts(v("UP"), v("UP"), col(3), A.add)
+    dma("Y", "d5", T.yu[:, S:W], T.UP[:, :], [v("UP")], [])
+    for e, n in sorted(count.items()):
+        g.wait_ge(T.sem[SEM.get(e, e[1:])], n)

@@ -1,6 +1,6 @@
-from concourse.mybir import AluOpType, AxisListType, ActivationFunctionType
+from concourse.mybir import AluOpType, ActivationFunctionType
 
-NB, NA, S, W, R = 32, 6, 4096, 4384, 3
+NB, NA, S, W, R, NS = 32, 6, 4096, 4384, 3, 22
 ZC, UW = 4608, 4624
 SG = (1, 9)
 F, B, I, H, U16 = "float32", "bfloat16", "int32", "float16", "uint16"
@@ -14,13 +14,13 @@ for _n in range(8):
     SCRATCH["p%d" % _n] = ("psum", [128, 512], F)
 for _w, _d, _s in (
         (UW, B, "U Tw FL"), (288, B, "UP"), (32, I, "CR"), (2048, B, "E2 E3 FX FD EH EL E1 LQ"), (2048, H, "WU WV KD"), (16384, B, "EQ"),
-        (512, F, "KD2 ior DA DB KA KB YC"), (2, I, "pi pq hwi"), (1, I, "kmi thi Pi Pj"), (1, F, "pf qf gf kmf thf"), (2, F, "hwf hwg hws hwm"),
+        (512, F, "ior YC"), (544, F, "KD2 DA DB"), (1088, F, "KAB"), (102, F, "KE"), (512, B, "LJ"), (48, F, "la"), (2, I, "pi pq hwi"), (1, I, "kmi thi Pi Pj"), (1, F, "pf qf gf kmf thf"), (2, F, "hwf hwg hws hwm"),
         (16, F, "io16 qm ql kq KM KS0 KS dA dB dC"), (16, I, "ki ka kb"), (128, F, "io8 io128 iox BF x1 x2 x3 x4 x5 x6 rep"), (128, B, "BD ID NI GE BH BL ZM"), (128, F, "O16"),
-        (96, F, "msk CA CB Hd"), (32, F, "col tc tcq tc512 tc1024 tc4096 W40 W4 on idx T1 nf pen0 pen cum s1 OF lf hx hx0 wl ld hm lo l2 Cf cw ee ec mu rc pj pj2 fo jt jj a1 a2 a3 a4 a5 a6 a7 n1 n2 n3 n4 n5"),
-        (32, I, "PR qi kk ks k2 k3 Hh Ci f3 fi nx Ai"), (64, I, "uva uv kI kJ dg"), (32, H, "uh qh hh"), (6, H, "ha"), (64, B, "dh dn"), (32, B, "pw wv"),
+        (96, F, "msk Hd Hj"), (32, F, "col tc tcq tc512 tc1024 tc4096 W40 W4 on idx T1 nf pen0 pen cum s1 OF lf hx hx0 hc wn wm wl ld hm lo l2 Cf cw ee ec mu rc pj pj2 fo jt jj a1 a2 a3 a4 a5 a6 a7 n1 n2 n3 n4 n5"),
+        (32, I, "PR qi k3 k4 Hh Ci f3 fi nx Ai"), (64, I, "uva kI kJ k2 dg"), (96, I, "uv"), (32, H, "uh qh hh"), (6, H, "ha"), (64, B, "dh dn"), (32, B, "pw wv"),
         (32, U16, "OFu lou fou JJ JB ngu"), (8, U16, "glu sou"), (64, U16, "CL"), (512, U16, "HL HR"), (512, I, "X X2"),
         (512, B, "JV L255 NB2 NG ZA Z TC GS LS JS DF0 DF1 DF2"), (1024, B, "JP NW JW AB0 AB1 AB2"), (528, B, "NR"), (1536, B, "ZS TS"), (384, B, "z4"), (576, F, "EA"),
-        (8, F, "la rA rB k6 k7 gt gl gm gm0 gn go gp gh"), (48, F, "t48 v48"), (24, F, "t24 v24"), (12, F, "t12 v12"), (192, B, "SB"), (96, B, "SU xt")):
+        (8, F, "k6 k7 gt gl gm gm0 gn go gp gh"), (192, B, "SB"), (96, B, "SU xt")):
     for _n in _s.split():
         if _w <= 64 and _n not in ("CR", "hwi", "kmi", "thi"):
             _k = "pk" + _d
@@ -36,7 +36,7 @@ def rank_program(g, core, T, topo):
     rank = T.rank_of(core)
     if rank is None:
         return
-    A, AF, X = AluOpType, ActivationFunctionType, AxisListType.X
+    A, AF = AluOpType, ActivationFunctionType
     Q = {"V": g.vector, "S": g.scalar, "P": g.tensor, "G": g, "Y": g.sync}
     SEM = {"V": "sv", "S": "ss", "P": "sp", "G": "sg"}
     count, known, snaps, rec = {}, {q: {} for q in Q}, {}, {}
@@ -151,6 +151,16 @@ def rank_program(g, core, T, topo):
             kw["bias"] = _(bias)
         op("S", lambda: g.scalar.activation(_(o), _(i), func, **kw), [i, scale, bias], [o])
 
+    def add_up(o, i, total):
+        op("S", lambda: g.scalar.activation(_(o), _(i), AF.Copy, accum_out=_(total)), [i], [o, total])
+
+    def weave(a, b, lead=0):
+        for k in range(lead):
+            next(a, None)
+        more = [a, b]
+        while more:
+            more = [x for x in more if next(x, more) is not more]
+
     def mm(o, l, r, start=True, stop=True):
         op("P", lambda: g.tensor.matmul(_(o), _(l), _(r), start, stop), [l, r], [o])
 
@@ -193,8 +203,8 @@ def rank_program(g, core, T, topo):
     iota(v("io16"), [[1, 16]], 0, 0)
     iota(v("io8"), [[1, 8], [0, 16]], 0, 0)
     iota(v("iox"), [[0, 8], [1, 16]], 0, 0)
-    iota(v("io128"), [[1, 128]], 0, 0)
     iota(v("E2"), [[-1, 16], [32, 8], [1, 16]], 0, 0)
+    iota(v("io128"), [[1, 128]], 0, 0)
     iota(v("E3"), [[1, 16], [32, 8], [0, 16]], 0, 0)
     iota(v("tc"), [[16, 32]], 0, 0)
     iota(v("ior"), [[1, 512]], -256, 0)
@@ -233,14 +243,16 @@ def rank_program(g, core, T, topo):
     ts(col(13), v("gf"), 32.0, A.mult)
     tt(col(14), col(13), v("qf"), A.add)
     ts(v("FX"), v("E2"), col(13), A.is_equal, col(15), A.mult)
+    for j in (0, 1):
+        for q in range(16):
+            mm(v("p0", 32 * j, 32 * j + 32), mat("FX", q), v("NR", j + q, j + 512, 16), q == 0, q == 15)
     ts(v("BF"), v("io8"), v("gf"), A.is_equal)
     ts(col(1), col(0), -512.0, A.mult, 256.0, A.add)
     ts(col(2), col(0), -256.0, A.mult)
     ts(col(3), col(0), 256.0, A.mult)
     ts(col(5), col(0), -256.0, A.mult, 255.0, A.add)
     ts(col(6), v("qm", 1, 2), -512.0, A.mult)
-    for n, lo, hi in (("Tw", S, UW), ("U", S, ZC)):
-        ms(v(n, lo, hi), 0.0)
+    ms(v("Tw", S, UW), 0.0)
     cp(v("hwf"), v("hwi"))
     ts(v("hwg"), v("hwf"), 2048.0, A.is_ge, -4096.0, A.mult)
     tt(v("hws"), v("hwg"), v("hwf"), A.add)
@@ -252,13 +264,12 @@ def rank_program(g, core, T, topo):
     ts(v("WU"), v("E2"), col(13), A.is_equal, v("hws", 0, 1), A.mult)
     cp(v("col", 7, 9), v("p5", 0, 2))
     cp(v("KM"), v("p5", 2, 18))
-    ts(v("WV"), v("E2"), col(13), A.is_equal, v("hws", 1, 2), A.mult)
-    ts(v("ID"), v("io128"), v("pf"), A.is_equal)
-    ts(v("KS0"), v("KM"), 2048.0, A.is_ge, -4096.0, A.mult)
-    tt(v("KS"), v("KS0"), v("KM"), A.add)
-    ts(v("U", ZC, UW), v("Tw", ZC, UW), col(2), A.add)
 
     def setup_hash():
+        ts(v("WV"), v("E2"), col(13), A.is_equal, v("hws", 1, 2), A.mult)
+        ts(v("KS0"), v("KM"), 2048.0, A.is_ge, -4096.0, A.mult)
+        ts(v("ID"), v("io128"), v("pf"), A.is_equal)
+        tt(v("KS"), v("KS0"), v("KM"), A.add)
         for m in range(16):
             ts(mat("KD", m), v("ID"), v("KS", m, m + 1), A.mult)
         ts(v("NI"), v("ID"), -1.0, A.mult)
@@ -271,6 +282,10 @@ def rank_program(g, core, T, topo):
         act(v("L255"), v("E2", 0, 512), AF.Identity, scale=0.0, bias=col(5))
 
     def setup_late():
+        ms(v("U", S, ZC), 0.0)
+        ts(v("U", ZC, UW), v("Tw", ZC, UW), col(2), A.add)
+        cp(v("Cf"), v("idx"))
+        cp(v("Ci"), v("idx"))
         ts(v("FD"), v("E2"), col(13), A.is_equal, 4096.0, A.mult)
         cp(v("ki"), v("KM"))
         ts(v("ka"), v("ki"), 4, A.arith_shift_right)
@@ -281,15 +296,16 @@ def rank_program(g, core, T, topo):
 
     def setup_last():
         yield
-        for d, D, C in (("dA", "DA", "CA"), ("dB", "DB", "CB")):
+        for d, D in (("dA", "DA"), ("dB", "DB")):
             tt(v(D, 1, 16), v(d, 0, 15), v(d, 1, 16), A.subtract)
             ms(v(D, 0, 1), 33554432.0)
-            w = 16
-            while w < 512:
+            cp(v(D, 16, 17), v(d, 15, 16))
+            w = 17
+            while w < 544:
                 act(v(D, w, 2 * w), v(D, 0, w))
                 w *= 2
-            for b in range(NA):
-                cp(v(C, b, 96, NA), v(d))
+        ms(v("KD2", 16, 544, 17), 67108864.0)
+        ms(v("KE", 16, 102, 17), 67108864.0)
         yield
         ts(v("rep", p=slice(0, 8)), v("io8", p=slice(0, 8)), v("pf", p=slice(0, 8)), A.is_equal)
         cp(v("thf", p=slice(0, 8)), v("thi", p=slice(0, 8)))
@@ -305,7 +321,6 @@ def rank_program(g, core, T, topo):
         ts(v("W4"), v("W40"), 4.0, A.add)
         cp(col(9), v("p5", 0, 1))
         ts(col(10), col(9), 4081.0, A.min, 4096.0, A.mult)
-        tt(col(11), col(10), v("dA", 15, 16), A.subtract)
         yield
         ms(v("O16"), 0.0625)
         ms(v("ZM"), 0.0)
@@ -341,36 +356,87 @@ def rank_program(g, core, T, topo):
 
     def hash_uv(nb):
         ts(v("uva", 0, nb), v("p0", 0, nb), col(7), A.add)
+        yield
         ts(v("uva", nb, 2 * nb), v("p0", 32, 32 + nb), col(8), A.add)
-        ts(v("uv", 0, 2 * nb), v("uva", 0, 2 * nb), 4095, A.bitwise_and)
-        tt(v("PR", 0, nb), v("uv", 0, nb), v("uv", nb, 2 * nb), A.mult)
-        ts(v("T1", 0, nb), v("uv", 0, nb), 2048.0, A.is_ge, -4096.0, A.mult)
+        yield
+        ts(v("uv", nb, 3 * nb), v("uva", 0, 2 * nb), 4095, A.bitwise_and)
+        yield
+        tt(v("PR", 0, nb), v("uv", nb, 2 * nb), v("uv", 2 * nb, 3 * nb), A.mult)
+        yield
+        ts(v("T1", 0, nb), v("uv", nb, 2 * nb), 2048.0, A.is_ge, -4096.0, A.mult)
+        yield
         ts(v("qi", 0, nb), v("PR", 0, nb), 5, A.arith_shift_right, 4095, A.bitwise_and)
-        tt(v("uh", 0, nb), v("T1", 0, nb), v("uv", 0, nb), A.add)
+        yield
+        tt(v("uh", 0, nb), v("T1", 0, nb), v("uv", nb, 2 * nb), A.add)
+        yield
         ts(v("qh", 0, nb), v("qi", 0, nb), -2048.0, A.add)
+        yield
+        ts(v("uv", 0, nb), v("uv", nb, 2 * nb), 16.0, A.mult)
+        yield
 
-    def hash_lists(nb, half):
-        ps = "p3" if half else "p1"
-        for m in range(8 * half, 8 * half + 8):
-            o = v(ps, (m - 8 * half) * nb, (m - 8 * half) * nb + nb)
+    def hash_lists(nb, ps, lo, hi):
+        for m in range(lo, hi):
+            o = v(ps, (m - lo) * nb, (m - lo) * nb + nb)
             mm(o, mat("KD", m), v("uh", 0, nb), True, False)
             mm(o, v("ID"), v("qh", 0, nb), False, True)
 
-    def lists(half, nb):
-        w, o = 8 * nb, 8 * nb * half
-        ts(v("X", o, o + w), v("p3" if half else "p1", 0, w), 2048.0, A.add)
+    def lists(ps, at, o, w):
+        ts(v("X", o, o + w), v(ps, at, at + w), 2048.0, A.add)
+        yield
         ts(v("X2", o, o + w), v("X", o, o + w), 4095, A.bitwise_and)
+        yield
         cp(v("HL", o, o + w), v("X2", o, o + w))
+        yield
 
-    def best(nb, ka, da, kb, db):
-        ts(v("kI", 0, nb), ka, da, A.add)
-        ts(v("kI", nb, 2 * nb), kb, db, A.add)
+    def best(nb, keys):
+        cp(v("kI", 0, 2 * nb), keys)
+        yield
         ts(v("kJ", 0, 2 * nb), v("kI", 0, 2 * nb), 255, A.bitwise_and)
-        ts(v("kk", 0, nb), v("kJ", 0, nb), 16.0, A.mult)
-        tt(v("ks", 0, nb), v("kk", 0, nb), v("kJ", nb, 2 * nb), A.add)
-        tt(v("k2", 0, nb), v("ks", 0, nb), v("uv", 0, nb), A.mult)
-        tt(v("k3", 0, nb), v("k2", 0, nb), v("qi", 0, nb), A.add)
-        ts(v("Hh", 0, nb), v("k3", 0, nb), 4095, A.bitwise_and)
+        yield
+        tt(v("k2", 0, 2 * nb), v("kJ", 0, 2 * nb), v("uv", 0, 2 * nb), A.mult)
+        yield
+        tt(v("k3", 0, nb), v("k2", 0, nb), v("k2", nb, 2 * nb), A.add)
+        yield
+        tt(v("k4", 0, nb), v("k3", 0, nb), v("qi", 0, nb), A.add)
+        yield
+        ts(v("Hh", 0, nb), v("k4", 0, nb), 4095, A.bitwise_and)
+        yield
+
+    def poor():
+        ts(v("nf"), v("KAB", 16, 544, 17), col(10), A.is_ge)
+        yield
+        tt(v("pw"), v("nf"), v("mu"), A.mult)
+        mm(v("p5", 0, 32), v("BD"), v("pw"))
+        mm(v("p5", 32, 64), v("GE"), v("pw"))
+        yield
+        ts(v("pen0"), v("pw"), 0.5, A.is_lt)
+        yield
+        tt(v("lf"), v("rc"), v("nf"), A.is_gt)
+        yield
+        tt(v("pen"), v("pen0"), v("tc1024"), A.mult)
+        yield
+        scan(v("cum"), v("on"), v("p5", 0, 32), 0.0, A.mult, A.add)
+        yield
+        ts(v("hx0"), v("lf"), -8192.0, A.mult, 8192.0 - 2048.0, A.add)
+        yield
+        tt(v("s1"), v("cum"), v("p5", 32, 64), A.subtract)
+        yield
+        tt(v("OF"), v("s1"), v("pen"), A.max)
+        yield
+        cp(v("OFu"), v("OF"))
+        yield
+
+    def laid():
+        ts(v("wl"), v("p5", 192, 224), 0.5, A.is_lt)
+        yield
+        tt(v("ld"), v("wl"), v("wm"), A.mult)
+        yield
+        tt(v("lo"), v("ld"), v("hm"), A.mult)
+        yield
+        tt(v("l2"), v("lo"), v("tc4096"), A.add)
+        yield
+        cp(v("lou"), v("l2"))
+        yield
 
     def widths():
         ts(v("f3"), v("Ci"), 3, A.bitwise_and)
@@ -414,10 +480,15 @@ def rank_program(g, core, T, topo):
         to_list(v("p4", 96, 128), "NG")
         yield
         ts(v("n1"), v("p4", 96, 128), 0.5, A.is_ge)
+        yield
         tt(v("n3"), v("n1"), v("n2"), A.mult)
+        yield
         tt(v("n5"), v("n3"), v("n4"), A.mult)
+        yield
+        tt(v("Ci"), v("n5"), v("idx"), A.add)
+        yield
         tt(v("Cf"), v("n5"), v("idx"), A.add)
-        cp(v("Ci"), v("Cf"))
+        yield
         digits(v("Ci"), "dn")
         yield
         rows("dn")
@@ -457,7 +528,7 @@ def rank_program(g, core, T, topo):
     def take(k):
         bank, o = "p7" if k % 2 else "p2", 64 * (k // 2)
         for j in (0, 1):
-            act(v("KD2", 2 * k + j, 512, 16), v(bank, o + 32 * j, o + 32 * j + 32))
+            act(v("KD2", 2 * k + j, 544, 17), v(bank, o + 32 * j, o + 32 * j + 32))
 
     def side(t):
         for x in (numbers(t - 1) if t else setup_last()):
@@ -465,17 +536,12 @@ def rank_program(g, core, T, topo):
         for x in widths():
             yield
 
-    next_lists()
     for t in range(R):
         last = t == R - 1
         lender, asker = T.cores[(rank + 1 + t) % 8], T.cores[(rank - 1 - t) % 8]
         cp(v("CL"), v("p0", 0, 64))
         if t == 0:
             cp(v("idx"), v("p0", 0, 32))
-            setup_hash()
-            cp(v("Cf"), v("idx"))
-            cp(v("Ci"), v("idx"))
-            setup_fill()
         else:
             tt(v("xt"), v("RB%d" % (t - 1), 96, 192), v("TS", 0, 96), A.mult)
             tt(v("Tw", S + 96 * t - 96, S + 96 * t), v("xt"), v("RB%d" % (t - 1), 0, 96), A.add)
@@ -485,19 +551,27 @@ def rank_program(g, core, T, topo):
             next(todo, None)
         tt(v("Z"), ind(v("Tw", 0, W), v("CL", 32, 64)), v("ZA"), A.min)
         if t == 0:
+            setup_hash()
             for k in range(4):
                 u_fix(k, 2)
+            setup_fill()
         hash_sums("Z", NB)
         if t:
             next(todo, None)
-        hash_uv(NB)
-        hash_lists(NB, 0)
-        hash_lists(NB, 1)
+        if t:
+            weave(hash_uv(NB), (next(todo, None) for k in range(5)), 4)
+        else:
+            for x in hash_uv(NB):
+                pass
+        hash_lists(NB, "p1", 0, 8)
+        hash_lists(NB, "p3", 8, 16)
         if t == 0:
             setup_late()
         else:
             next(todo, None)
-        lists(0, NB)
+        for x in lists("p1", 0, 0, 128):
+            pass
+        more = [lists("p3" if k > 1 else "p1", 128 * (k % 2), 128 * k, 128) for k in (1, 2, 3)]
         gather(SG[0])
         ready = []
         for i, m in enumerate([m for m in range(16) if m not in SG]):
@@ -513,9 +587,9 @@ def rank_program(g, core, T, topo):
                 mm(v("p4"), v("NI"), v("Z"), False, True)
                 act(diff_of(m + 1), v("p4"), AF.Abs)
                 done = [m // 2]
-            if i == 4:
-                lists(1, NB)
-            if i == 5:
+            if i < 9:
+                next(more[i // 3])
+            if i == 6:
                 gather(SG[1])
             if i >= 1:
                 next(todo, None)
@@ -527,28 +601,18 @@ def rank_program(g, core, T, topo):
         for k in ready:
             take(k)
         slots()
-        scan(v("KA"), v("DA"), v("KD2"), 0.0, A.add, A.min)
-        ts(v("nf"), v("KA", 15, 512, 16), col(11), A.is_ge)
-        tt(v("pw"), v("nf"), v("mu"), A.mult)
-        mm(v("p5", 0, 32), v("BD"), v("pw"))
-        mm(v("p5", 32, 64), v("GE"), v("pw"))
-        ts(v("pen0"), v("pw"), 0.5, A.is_lt)
-        tt(v("pen"), v("pen0"), v("tc1024"), A.mult)
-        scan(v("cum"), v("on"), v("p5", 0, 32), 0.0, A.mult, A.add)
-        tt(v("s1"), v("cum"), v("p5", 32, 64), A.subtract)
-        tt(v("OF"), v("s1"), v("pen"), A.max)
-        cp(v("OFu"), v("OF"))
-        cp(ind(v("ZS"), v("OFu")), v("Z"))
-        send("az%d" % t, "lz", lender, T["ZR%d" % t][:, :], T.ZS[:, 0:96], [v("ZS", 0, 96)])
-        scan(v("KB"), v("DB"), v("KD2"), 0.0, A.add, A.min)
-        best(NB, v("KA", 15, 512, 16), v("dA", 15, 16), v("KB", 15, 512, 16), v("dB", 15, 16))
-        ts(v("hh"), v("Hh"), -2048.0, A.add)
+        scan(v("KAB", 0, 544), v("DA"), v("KD2"), 0.0, A.add, A.min)
+        scan(v("KAB", 544, 1088), v("DB"), v("KD2"), 0.0, A.add, A.min)
+        weave(best(NB, v("KAB", 16, 1088, 17)), poor())
+        tt(v("hh"), v("hx0"), v("Hh"), A.add)
+        tt(v("hx"), v("hx0"), v("Hh"), A.add)
         for q in range(16):
             mm(v("p1", q, 512, 16), mat("E1", q), v("hh"))
+        cp(ind(v("ZS"), v("OFu")), v("Z"))
+        send("az%d" % t, "lz", lender, T["ZR%d" % t][:, :], T.ZS[:, 0:96], [v("ZS", 0, 96)])
         mm(v("p7"), v("ZM"), v("Z"), True, False)
-        tt(v("lf"), v("rc"), v("nf"), A.is_gt)
-        ts(v("hx0"), v("lf"), -60000.0, A.mult, 60000.0, A.add)
-        tt(v("hx"), v("hx0"), v("Hh"), A.add)
+        ts(v("hc"), v("hx"), 2048.0, A.add)
+        cp(v("wm", 0, NS), v("lf", 0, NS))
         tt(v("hm"), v("Hh"), v("tc4096"), A.subtract)
         tt(v("a1"), v("Hh"), v("Cf"), A.subtract)
         if not last:
@@ -556,11 +620,15 @@ def rank_program(g, core, T, topo):
         if t:
             put_numbers(t - 1)
         ts(v("HR"), v("p1"), 2048.0, A.add)
-        for b in range(NB):
+        for b in range(NS, NB):
             e = 512 * b
-            ts(v("EQ", e, e + 512 - 16 * b), v("HR", 16 * b, 512), v("hx", b, b + 1), A.is_equal)
-            if b < NB - 1:
-                mm(v("p7", 16 * b + 16, 512), v("BD"), v("EQ", e + 16, e + 512 - 16 * b), False, False)
+            ts(v("EQ", e - 16 * b, e + 16), v("HR", 0, 16 * b + 16), v("hc", b, b + 1), A.is_equal)
+            add_up(v("LJ", 0, 16 * b), v("EQ", e - 16 * b, e), v("la", b, b + 1))
+        for b in range(NS):
+            e, w = 512 * b, 16 * NS - 16 * b
+            ts(v("EQ", e, e + w), v("HR", 16 * b, 16 * NS), v("hc", b, b + 1), A.is_equal)
+            if b < NS - 1:
+                mm(v("p7", 16 * b + 16, 16 * NS), v("BD"), v("EQ", e + 16, e + w), False, False)
         for q in range(1, 16):
             mm(v("p7", q, 512, 16), mat("LQ", q), v("EQ", q, 15872 + q + 1, 512), False, q == 15)
         act(v("LS"), v("p7"))
@@ -574,19 +642,15 @@ def rank_program(g, core, T, topo):
         slots_lists()
         if not last:
             cp(ind(v("TS"), v("OFu")), v("TC"))
-        hash_uv(NA)
-        hash_lists(NA, 0)
-        hash_lists(NA, 1)
-        ts(v("wl"), v("p5", 192, 224), 0.5, A.is_lt)
-        tt(v("ld"), v("wl"), v("lf"), A.mult)
-        tt(v("lo"), v("ld"), v("hm"), A.mult)
-        tt(v("l2"), v("lo"), v("tc4096"), A.add)
-        cp(v("lou"), v("l2"))
+        ts(v("wn", NS, NB), v("la", NS, NB), 0.5, A.is_lt)
+        tt(v("wm", NS, NB), v("wn", NS, NB), v("lf", NS, NB), A.mult)
+        weave(hash_uv(NA), laid(), 4)
+        hash_lists(NA, "p1", 0, 16)
         cp(ind(v("U", 0, ZC), v("lou")), v("L255"))
         if not last:
             cp(v("Pi"), v("p5", 224, 225))
-        lists(0, NA)
-        lists(1, NA)
+        for x in lists("p1", 0, 0, 96):
+            pass
         for k in range(4):
             df, ab, o = "DF%d" % (k % 3), "AB%d" % (k // 2), 384 * (k % 2)
             tt(v(df, 0, 384), ind(v("U", 0, S), v("HL", 24 * k, 24 * k + 24)), v("z4"), A.subtract)
@@ -594,6 +658,8 @@ def rank_program(g, core, T, topo):
             if k % 2:
                 for q in range(16):
                     mm(v("p2", 48 * (k // 2), 48 * (k // 2) + 48), mat("FD", q), v(ab, q, 768, 16), q == 0, q == 15)
+        for b in range(NA):
+            act(v("KE", 17 * b, 17 * b + 16), v("p2", b, 96, NA))
         tt(v("a2"), v("a1"), v("ld"), A.mult)
         ts(v("a3"), v("OF"), 95.5, A.is_lt)
         ts(v("a4"), v("OF"), float(S + 96 * t), A.add)
@@ -606,21 +672,21 @@ def rank_program(g, core, T, topo):
         slots2()
         act(v("NW", 0, 512), v("p6"))
         act(v("NR", 0, 512), ind(v("NW"), v("JJ")))
-        tt(v("KA", 0, 96), v("p2", 0, 96), v("CA"), A.add)
-        tt(v("KB", 0, 96), v("p2", 0, 96), v("CB"), A.add)
-        a, b_ = ("KA", 96), ("KB", 96)
-        for na, nb_, w in (("t48", "v48", 48), ("t24", "v24", 24), ("t12", "v12", 12), ("rA", "rB", 6)):
-            tt(v(na, 0, w), v(a[0], 0, w), v(a[0], w, 2 * w), A.min)
-            tt(v(nb_, 0, w), v(b_[0], 0, w), v(b_[0], w, 2 * w), A.min)
-            a, b_ = (na, w), (nb_, w)
-        best(NA, v("rA", 0, NA), 0.0, v("rB", 0, NA), 0.0)
-        ts(v("k6", 0, NA), v("rA", 0, NA), col(10), A.is_ge, 8192.0, A.mult)
+        scan(v("KAB", 0, 102), v("DA", 0, 102), v("KE"), 0.0, A.add, A.min)
+        scan(v("KAB", 102, 204), v("DB", 0, 102), v("KE"), 0.0, A.add, A.min)
+        key = v("KAB", 16, 102, 17)
+
+        def fits():
+            ts(v("k6", 0, NA), key, col(10), A.is_ge, 8192.0, A.mult)
+            yield
+            ts(v("gt", 0, NA), key, col(10), A.is_lt)
+            yield
+        weave(best(NA, v("KAB", 16, 204, 17)), fits(), 1)
         ts(v("k7", 0, NA), v("Hh", 0, NA), -2048.0, A.add)
         tt(v("ha"), v("k6", 0, NA), v("k7", 0, NA), A.add)
         for q in range(16):
             mm(v("p1", q, 96, 16), mat("E1", q), v("ha"))
         next_lists()
-        ts(v("gt", 0, NA), v("rA", 0, NA), col(10), A.is_lt)
         ts(v("gh", 0, NA), v("Hh", 0, NA), float(-ZC), A.add)
         tt(v("gn", 0, NA), v("Hh", 0, NA), v("tc4096", 0, NA), A.subtract)
         tt(v("Hd"), v("p1", 0, 96), v("msk"), A.add)
@@ -628,10 +694,8 @@ def rank_program(g, core, T, topo):
             if b:
                 ts(v("EA", 96 * b, 96 * b + 16 * b), v("p1", 0, 16 * b), v("k7", b, b + 1), A.is_equal)
             ts(v("EA", 112 * b, 112 * b + 16), v("Hd", 16 * b, 16 * b + 16), v("k7", b, b + 1), A.is_equal)
-        for b in range(NA):
-            o, x = v("la", b, b + 1), v("EA", 96 * b, 112 * b + 16)
-            op("V", lambda: g.vector.tensor_reduce(_(o), _(x), X, A.add), [x], [o])
-        ts(v("gm0", 0, NA), v("la", 0, NA), 0.5, A.is_lt)
+            add_up(v("Hj", 0, 16 * b + 16), v("EA", 96 * b, 112 * b + 16), v("la", 32 + b, 33 + b))
+        ts(v("gm0", 0, NA), v("la", 32, 32 + NA), 0.5, A.is_lt)
         tt(v("gm", 0, NA), v("gm0", 0, NA), v("gt", 0, NA), A.mult)
         tt(v("gl", 0, NA), v("gm", 0, NA), v("gh", 0, NA), A.mult)
         ts(v("glu", 0, NA), v("gl", 0, NA), float(ZC), A.add)
@@ -652,7 +716,6 @@ def rank_program(g, core, T, topo):
             ts(v("Pj"), v("Pi"), 63, A.bitwise_and)
             tt(col(16), col(9), v("Pj"), A.add)
             ts(col(10), col(16), 4081.0, A.min, 4096.0, A.mult)
-            tt(col(11), col(10), v("dA", 15, 16), A.subtract)
             ms(v("ZS", 0, 96), 1024.0)
         base = float(S + 96 * t)
         cp(v("idx"), v("p0", 0, 32))

from concourse.mybir import AluOpType, ActivationFunctionType

NB, NA, S, W, R, NS = 32, 6, 4096, 4384, 3, 22
ZC, UW = 4608, 4624
SG = (1, 9)
F, B, I, H, U16 = "float32", "bfloat16", "int32", "float16", "uint16"
SCRATCH, PACK, PACKED = {}, {}, {}
SEMAPHORES = ["sv", "ss", "sp", "sg", "d0", "d1", "d2", "d3", "d4", "d5", "dt", "lz", "ly", "lx"] + ["du%d" % t for t in range(4)]
for _t in range(R):
    SEMAPHORES += ["az%d" % _t, "ar%d" % _t, "au%d" % _t]
    SCRATCH["ZR%d" % _t] = ("sbuf", [128, 96], B)
    SCRATCH["RB%d" % _t] = ("sbuf", [128, 192], B)
for _n in range(8):
    SCRATCH["p%d" % _n] = ("psum", [128, 512], F)
for _w, _d, _s in (
        (UW, B, "U Tw FL"), (288, B, "UP"), (32, I, "CR"), (2048, B, "E2 E3 FX FD EH EL E1 LQ"), (2048, H, "WU WV KD"), (16384, B, "EQ"),
        (512, F, "ior YC"), (544, F, "KD2 DA DB"), (1088, F, "KAB"), (102, F, "KE"), (512, B, "LJ"), (48, F, "la"), (2, I, "pi pq hwi"), (1, I, "kmi thi Pi Pj"), (1, F, "pf qf gf kmf thf"), (2, F, "hwf hwg hws hwm"),
        (16, F, "io16 qm ql kq KM KS0 KS dA dB dC"), (16, I, "ki ka kb"), (128, F, "io8 io128 iox BF x1 x2 x3 x4 x5 x6 rep"), (128, B, "BD ID NI GE BH BL ZM"), (128, F, "O16"),
        (96, F, "msk Hd Hj"), (32, F, "col tc tcq tc512 tc1024 tc4096 W40 W4 on idx T1 nf pen0 pen cum s1 OF lf hx hx0 hc wn wm wl ld hm lo l2 Cf cw ee ec mu rc pj pj2 fo jt jj a1 a2 a3 a4 a5 a6 a7 n1 n2 n3 n4 n5"),
        (32, I, "PR qi k3 k4 Hh Ci f3 fi nx Ai"), (64, I, "uva kI kJ k2 dg"), (96, I, "uv"), (32, H, "uh qh hh"), (6, H, "ha"), (64, B, "dh dn"), (32, B, "pw wv"),
        (32, U16, "OFu lou fou JJ JB ngu"), (8, U16, "glu sou"), (64, U16, "CL"), (512, U16, "HL HR"), (512, I, "X X2"),
        (512, B, "JV L255 NB2 NG ZA Z TC GS LS JS DF0 DF1 DF2"), (1024, B, "JP NW JW AB0 AB1 AB2"), (528, B, "NR"), (1536, B, "ZS TS"), (384, B, "z4"), (576, F, "EA"),
        (8, F, "k6 k7 gt gl gm gm0 gn go gp gh"), (192, B, "SB"), (96, B, "SU xt")):
    for _n in _s.split():
        if _w <= 64 and _n not in ("CR", "hwi", "kmi", "thi"):
            _k = "pk" + _d
            PACK[_n] = (_k, PACKED.get(_k, 0), _w)
            PACKED[_k] = PACKED.get(_k, 0) + (_w + 7) // 8 * 8
        else:
            SCRATCH[_n] = ("sbuf", [128, _w], _d)
for _k, _w in PACKED.items():
    SCRATCH[_k] = ("sbuf", [128, _w], _k[2:])


def rank_program(g, core, T, topo):
    rank = T.rank_of(core)
    if rank is None:
        return
    A, AF = AluOpType, ActivationFunctionType
    Q = {"V": g.vector, "S": g.scalar, "P": g.tensor, "G": g, "Y": g.sync}
    SEM = {"V": "sv", "S": "ss", "P": "sp", "G": "sg"}
    count, known, snaps, rec = {}, {q: {} for q in Q}, {}, {}

    def v(name, lo=None, hi=None, step=1, p=None):
        buf, at, w = PACK[name] if name in PACK else (name, 0, SCRATCH[name][1][1])
        lo = 0 if lo is None else lo
        hi = w if hi is None else hi
        rows = slice(None) if p is None else p
        ap = T[buf][rows, at + lo:at + hi] if step == 1 else T[buf][rows, at + lo:at + hi:step]
        return (ap, name, lo, hi, step)

    def ind(win, off):
        return (win[0].indirect(off[0]), (win, off))

    def parts(x):
        return list(x[1]) if len(x) == 2 else [x]

    def hit(a, b):
        if a[1] >= b[2] or b[1] >= a[2]:
            return False
        return not (a[3] == b[3] and a[3] > 1 and (a[1] - b[1]) % a[3])

    def is_bank(n):
        return n[0] == "p" and n[1:].isdigit()

    def reg(x):
        return (x[1], 0, 512, 1) if is_bank(x[1]) else (x[1], x[2], x[3], x[4])

    def learn(q, e, n):
        known[q][e] = max(known[q].get(e, 0), n)
        for e2, n2 in snaps.get((e, n), {}).items():
            known[q][e2] = max(known[q].get(e2, 0), n2)

    def settle(q, reads, writes):
        need = {}
        for xs, isw in ((reads, False), (writes, True)):
            for x in xs:
                r = reg(x)
                ps = is_bank(r[0])
                for (o, e, n, w) in rec.get(r[0], []):
                    if not hit(r, o):
                        continue
                    if e == q:
                        if q == "P" or not (w or isw):
                            continue
                    elif not (w or isw or ps):
                        continue
                    need[e] = max(need.get(e, 0), count[e] if e[0] in "DL" else n)
        for e, n in sorted(need.items(), key=lambda kv: -kv[1]):
            if known[q].get(e, 0) < n:
                Q[q].wait_ge(T.sem[SEM.get(e, e[1:])], n)
                learn(q, e, n)

    def note(e, n, reads, writes, snap):
        snaps[(e, n)] = dict(snap)
        for xs, isw in ((reads, False), (writes, True)):
            for x in xs:
                r = reg(x)
                old = rec.setdefault(r[0], [])
                if isw:
                    old[:] = [o for o in old if not (o[0][1] >= r[1] and o[0][2] <= r[2] and r[3] == 1)]
                old[:] = [o for o in old if not (o[0] == r and o[1] == e and o[3] == isw)]
                old.append((r, e, n, isw))

    def op(q, f, reads, writes):
        rs = [p for x in reads if isinstance(x, tuple) for p in parts(x)]
        ws = []
        for x in writes:
            ps = parts(x)
            ws.append(ps[0])
            rs += ps[1:]
        settle(q, rs, ws)
        count[q] = count.get(q, 0) + 1
        f().then_inc(T.sem[SEM[q]], 1)
        note(q, count[q], rs, ws, known[q])

    def dma(q, sem, out, in_, reads, writes):
        settle(q, reads, writes)
        e = "D" + sem
        count[e] = count.get(e, 0) + 16
        Q[q].dma_start(out, in_).then_inc(T.sem[sem], 16)
        note(e, count[e], reads, writes, known[q])

    def _(x):
        return x[0] if isinstance(x, tuple) else x

    def ts(o, i, s1, op0, s2=None, op1=None):
        rd = [i, s1, s2]
        if op1 is None:
            op("V", lambda: g.vector.tensor_scalar(out=_(o), in0=_(i), scalar1=_(s1), scalar2=None, op0=op0), rd, [o])
        else:
            op("V", lambda: g.vector.tensor_scalar(out=_(o), in0=_(i), scalar1=_(s1), scalar2=_(s2), op0=op0, op1=op1), rd, [o])

    def tt(o, a, b, op0):
        op("V", lambda: g.vector.tensor_tensor(out=_(o), in0=_(a), in1=_(b), op=op0), [a, b], [o])

    def cp(o, i):
        op("V", lambda: g.vector.tensor_copy(out=_(o), in_=_(i)), [i], [o])

    def ms(o, c):
        op("V", lambda: g.vector.memset(_(o), c), [], [o])

    def scan(o, a, b, init, op0, op1):
        op("V", lambda: g.vector.tensor_tensor_scan(_(o), _(a), _(b), init, op0, op1), [a, b], [o])

    def act(o, i, func=AF.Copy, scale=None, bias=None):
        kw = {}
        if scale is not None:
            kw["scale"] = _(scale)
        if bias is not None:
            kw["bias"] = _(bias)
        op("S", lambda: g.scalar.activation(_(o), _(i), func, **kw), [i, scale, bias], [o])

    def add_up(o, i, total):
        op("S", lambda: g.scalar.activation(_(o), _(i), AF.Copy, accum_out=_(total)), [i], [o, total])

    def weave(a, b, lead=0):
        for k in range(lead):
            next(a, None)
        more = [a, b]
        while more:
            more = [x for x in more if next(x, more) is not more]

    def mm(o, l, r, start=True, stop=True):
        op("P", lambda: g.tensor.matmul(_(o), _(l), _(r), start, stop), [l, r], [o])

    def iota(o, pattern, base, cm, flag=True):
        op("G", lambda: g.iota(_(o), pattern, base, cm, allow_small_or_imprecise_dtypes=True) if flag else g.iota(_(o), pattern, base, cm), [], [o])

    def col(j):
        return v("col", j, j + 1)

    def mat(name, q):
        return v(name, 128 * q, 128 * q + 128)

    def send(sem, lsem, dst, out, in_, reads):
        settle("G", reads, [])
        es = topo.engines(core, dst)[:8]
        rid, pid, se = topo.addr(dst)
        e = "L" + lsem
        count[e] = count.get(e, 0) + len(es)
        g.remote_dma(out, in_, T.sem[sem], T.sem[lsem], pid, rid, sum(1 << k for k in es))
        note(e, count[e], reads, [], known["G"])

    for t in range(R):
        asker, lender = T.cores[(rank - 1 - t) % 8], T.cores[(rank + 1 + t) % 8]
        for sem, src, ws in (("az%d" % t, asker, [v("ZR%d" % t)]), ("ar%d" % t, lender, [v("RB%d" % t)]), ("au%d" % t, lender, [v("UP", 96 * t, 96 * t + 96)])):
            n = len(topo.engines(src, core)[:8])
            count["A" + sem] = n
            note("A" + sem, n, [], ws, {})

    dma("Y", "d0", T.CR[:, :], T.c0[:, :], [], [v("CR")])
    dma("S", "d1", T.hwi[:, :], T.hw[:, :], [], [v("hwi")])
    dma("S", "d1", T.kmi[:, :], T.km[:, :], [], [v("kmi")])
    for k in range(16):
        lo = 8 * k
        dma("S" if k % 2 else "Y", "d2", T.Tw[lo:lo + 8, 0:S], T.tp[(lo ^ 8):(lo ^ 8) + 8, :], [], [v("Tw", 0, S)] if k == 15 else [])
    dma("Y", "dt", T.thi[0:8, :], T.th[:, :], [], [v("thi")])
    for k in range(4):
        dma("Y", "du%d" % k, T.U[:, 1024 * k:1024 * k + 1024], T.us[:, 1024 * k:1024 * k + 1024], [], [v("U", 1024 * k, 1024 * k + 1024)])

    iota(v("pi"), [[0, 2]], 0, 1, False)
    iota(v("io16"), [[1, 16]], 0, 0)
    iota(v("io8"), [[1, 8], [0, 16]], 0, 0)
    iota(v("iox"), [[0, 8], [1, 16]], 0, 0)
    iota(v("E2"), [[-1, 16], [32, 8], [1, 16]], 0, 0)
    iota(v("io128"), [[1, 128]], 0, 0)
    iota(v("E3"), [[1, 16], [32, 8], [0, 16]], 0, 0)
    iota(v("tc"), [[16, 32]], 0, 0)
    iota(v("ior"), [[1, 512]], -256, 0)
    iota(v("FL", 0, ZC), [[0, ZC]], 0, 0)
    iota(v("FL", ZC, UW), [[0, UW - ZC]], 1, 0)
    cp(v("pf"), v("pi", 0, 1))
    ts(v("pq", 0, 1), v("pi", 0, 1), 4, A.arith_shift_right)
    ts(v("pq", 1, 2), v("pi", 0, 1), 15, A.bitwise_and)
    cp(v("gf"), v("pq", 0, 1))
    cp(v("qf"), v("pq", 1, 2))
    ts(v("qm"), v("io16"), v("qf"), A.is_equal)
    ts(v("BD"), v("io8"), v("gf"), A.is_equal)
    ts(v("x1"), v("iox"), 2.0, A.is_equal, 128.0, A.mult)
    ts(v("x2"), v("iox"), 0.0, A.is_equal)
    tt(v("x3"), v("x1"), v("x2"), A.add)
    tt(v("BH"), v("x3"), v("BD"), A.mult)
    for q in range(16):
        act(mat("EH", q), v("BH"), scale=v("qm", q, q + 1))
    ts(v("x4"), v("iox"), 2.0, A.is_equal)
    ts(v("x5"), v("iox"), 1.0, A.is_equal)
    tt(v("x6"), v("x4"), v("x5"), A.add)
    tt(v("BL"), v("x6"), v("BD"), A.mult)
    for q in range(16):
        ts(mat("EL", q), v("BL"), v("qm", q, q + 1), A.mult)
    ts(v("dg", 0, 32), v("CR"), 7, A.arith_shift_right)
    ts(v("dg", 32, 64), v("CR"), 127, A.bitwise_and)
    cp(v("dh"), v("dg"))
    for q in range(16):
        mm(v("p6", 32 * q, 32 * q + 32), mat("EH", q), v("dh", 0, 32), True, False)
        mm(v("p6", 32 * q, 32 * q + 32), mat("EL", q), v("dh", 32, 64), False, True)
    ms(v("NR", 512, 528), 0.0)
    act(v("NR", 0, 512), v("p6"))
    ts(col(0), v("qf"), 7.5, A.is_lt)
    ts(col(4), v("qm", 0, 1), 128.0, A.mult)
    tt(col(15), col(4), v("qm", 1, 2), A.add)
    ts(col(13), v("gf"), 32.0, A.mult)
    tt(col(14), col(13), v("qf"), A.add)
    ts(v("FX"), v("E2"), col(13), A.is_equal, col(15), A.mult)
    for j in (0, 1):
        for q in range(16):
            mm(v("p0", 32 * j, 32 * j + 32), mat("FX", q), v("NR", j + q, j + 512, 16), q == 0, q == 15)
    ts(v("BF"), v("io8"), v("gf"), A.is_equal)
    ts(col(1), col(0), -512.0, A.mult, 256.0, A.add)
    ts(col(2), col(0), -256.0, A.mult)
    ts(col(3), col(0), 256.0, A.mult)
    ts(col(5), col(0), -256.0, A.mult, 255.0, A.add)
    ts(col(6), v("qm", 1, 2), -512.0, A.mult)
    ms(v("Tw", S, UW), 0.0)
    cp(v("hwf"), v("hwi"))
    ts(v("hwg"), v("hwf"), 2048.0, A.is_ge, -4096.0, A.mult)
    tt(v("hws"), v("hwg"), v("hwf"), A.add)
    ts(v("hwm"), v("hws"), col(3), A.mult)
    cp(v("kmf"), v("kmi"))
    ts(v("kq"), v("qm"), v("kmf"), A.mult)
    mm(v("p5", 0, 2), v("BF"), v("hwm"))
    mm(v("p5", 2, 18), v("BF"), v("kq"))
    ts(v("WU"), v("E2"), col(13), A.is_equal, v("hws", 0, 1), A.mult)
    cp(v("col", 7, 9), v("p5", 0, 2))
    cp(v("KM"), v("p5", 2, 18))

    def setup_hash():
        ts(v("WV"), v("E2"), col(13), A.is_equal, v("hws", 1, 2), A.mult)
        ts(v("KS0"), v("KM"), 2048.0, A.is_ge, -4096.0, A.mult)
        ts(v("ID"), v("io128"), v("pf"), A.is_equal)
        tt(v("KS"), v("KS0"), v("KM"), A.add)
        for m in range(16):
            ts(mat("KD", m), v("ID"), v("KS", m, m + 1), A.mult)
        ts(v("NI"), v("ID"), -1.0, A.mult)

    def setup_fill():
        act(v("NW", 512, 1024), v("p6"))
        act(v("JV"), v("ior"), scale=v("qm", 1, 2))
        act(v("JP"), v("E2", 0, 1024), AF.Identity, scale=0.0, bias=col(6))
        act(v("JW"), v("JP"))
        act(v("L255"), v("E2", 0, 512), AF.Identity, scale=0.0, bias=col(5))

    def setup_late():
        ms(v("U", S, ZC), 0.0)
        ts(v("U", ZC, UW), v("Tw", ZC, UW), col(2), A.add)
        cp(v("Cf"), v("idx"))
        cp(v("Ci"), v("idx"))
        ts(v("FD"), v("E2"), col(13), A.is_equal, 4096.0, A.mult)
        cp(v("ki"), v("KM"))
        ts(v("ka"), v("ki"), 4, A.arith_shift_right)
        ts(v("kb"), v("ki"), 15, A.bitwise_and)
        ts(v("dC"), v("io16"), 256.0, A.mult)
        tt(v("dB"), v("dC"), v("kb"), A.add)
        tt(v("dA"), v("dC"), v("ka"), A.add)

    def setup_last():
        yield
        for d, D in (("dA", "DA"), ("dB", "DB")):
            tt(v(D, 1, 16), v(d, 0, 15), v(d, 1, 16), A.subtract)
            ms(v(D, 0, 1), 33554432.0)
            cp(v(D, 16, 17), v(d, 15, 16))
            w = 17
            while w < 544:
                act(v(D, w, 2 * w), v(D, 0, w))
                w *= 2
        ms(v("KD2", 16, 544, 17), 67108864.0)
        ms(v("KE", 16, 102, 17), 67108864.0)
        yield
        ts(v("rep", p=slice(0, 8)), v("io8", p=slice(0, 8)), v("pf", p=slice(0, 8)), A.is_equal)
        cp(v("thf", p=slice(0, 8)), v("thi", p=slice(0, 8)))
        mm(v("p5", 0, 1), v("rep", p=slice(0, 8)), v("thf", p=slice(0, 8)))
        ts(v("x1"), v("io128"), v("pf"), A.is_le)
        tt(v("GE"), v("x1"), v("BD"), A.mult)
        ms(v("on"), 1.0)
        ts(v("tcq"), v("tc"), v("qf"), A.add)
        yield
        for n in (512, 1024, 4096):
            ts(v("tc%d" % n), v("tcq"), float(n), A.add)
        ts(v("W40"), v("tcq"), 510.0, A.is_equal, 5112.0, A.mult)
        ts(v("W4"), v("W40"), 4.0, A.add)
        cp(col(9), v("p5", 0, 1))
        ts(col(10), col(9), 4081.0, A.min, 4096.0, A.mult)
        yield
        ms(v("O16"), 0.0625)
        ms(v("ZM"), 0.0)
        ts(v("ql"), v("io16"), v("qf"), A.is_gt)
        for q in range(1, 16):
            act(mat("LQ", q), v("BD"), scale=v("ql", q, q + 1))
        ms(v("ZS", 0, 96), 1024.0)
        ms(v("TS", 0, 96), 0.0)
        yield
        ts(v("E1"), v("E3"), col(14), A.is_equal)
        ts(v("msk"), v("iox", 0, 96), v("qf"), A.is_ge, 30000.0, A.mult)
        yield

    def to_list(ps, row, lo=0, n=512):
        for q in range(16):
            mm(ps, mat("FX", q), v(row, lo + q, lo + n, 16), q == 0, q == 15)

    def digits(src, name="dh"):
        ts(v("dg", 0, 32), src, 7, A.arith_shift_right)
        ts(v("dg", 32, 64), src, 127, A.bitwise_and)
        cp(v(name), v("dg"))

    def rows(name):
        for q in range(16):
            mm(v("p6", q, 512, 16), mat("EH", q), v(name, 0, 32), True, False)
            mm(v("p6", q, 512, 16), mat("EL", q), v(name, 32, 64), False, True)

    def hash_sums(z, nb):
        n = 16 * nb
        for j, w in ((0, "WU"), (1, "WV")):
            for q in range(16):
                mm(v("p0", 32 * j, 32 * j + nb), mat(w, q), v(z, q, n, 16), q == 0, q == 15)

    def hash_uv(nb):
        ts(v("uva", 0, nb), v("p0", 0, nb), col(7), A.add)
        yield
        ts(v("uva", nb, 2 * nb), v("p0", 32, 32 + nb), col(8), A.add)
        yield
        ts(v("uv", nb, 3 * nb), v("uva", 0, 2 * nb), 4095, A.bitwise_and)
        yield
        tt(v("PR", 0, nb), v("uv", nb, 2 * nb), v("uv", 2 * nb, 3 * nb), A.mult)
        yield
        ts(v("T1", 0, nb), v("uv", nb, 2 * nb), 2048.0, A.is_ge, -4096.0, A.mult)
        yield
        ts(v("qi", 0, nb), v("PR", 0, nb), 5, A.arith_shift_right, 4095, A.bitwise_and)
        yield
        tt(v("uh", 0, nb), v("T1", 0, nb), v("uv", nb, 2 * nb), A.add)
        yield
        ts(v("qh", 0, nb), v("qi", 0, nb), -2048.0, A.add)
        yield
        ts(v("uv", 0, nb), v("uv", nb, 2 * nb), 16.0, A.mult)
        yield

    def hash_lists(nb, ps, lo, hi):
        for m in range(lo, hi):
            o = v(ps, (m - lo) * nb, (m - lo) * nb + nb)
            mm(o, mat("KD", m), v("uh", 0, nb), True, False)
            mm(o, v("ID"), v("qh", 0, nb), False, True)

    def lists(ps, at, o, w):
        ts(v("X", o, o + w), v(ps, at, at + w), 2048.0, A.add)
        yield
        ts(v("X2", o, o + w), v("X", o, o + w), 4095, A.bitwise_and)
        yield
        cp(v("HL", o, o + w), v("X2", o, o + w))
        yield

    def best(nb, keys):
        cp(v("kI", 0, 2 * nb), keys)
        yield
        ts(v("kJ", 0, 2 * nb), v("kI", 0, 2 * nb), 255, A.bitwise_and)
        yield
        tt(v("k2", 0, 2 * nb), v("kJ", 0, 2 * nb), v("uv", 0, 2 * nb), A.mult)
        yield
        tt(v("k3", 0, nb), v("k2", 0, nb), v("k2", nb, 2 * nb), A.add)
        yield
        tt(v("k4", 0, nb), v("k3", 0, nb), v("qi", 0, nb), A.add)
        yield
        ts(v("Hh", 0, nb), v("k4", 0, nb), 4095, A.bitwise_and)
        yield

    def poor():
        ts(v("nf"), v("KAB", 16, 544, 17), col(10), A.is_ge)
        yield
        tt(v("pw"), v("nf"), v("mu"), A.mult)
        mm(v("p5", 0, 32), v("BD"), v("pw"))
        mm(v("p5", 32, 64), v("GE"), v("pw"))
        yield
        ts(v("pen0"), v("pw"), 0.5, A.is_lt)
        yield
        tt(v("lf"), v("rc"), v("nf"), A.is_gt)
        yield
        tt(v("pen"), v("pen0"), v("tc1024"), A.mult)
        yield
        scan(v("cum"), v("on"), v("p5", 0, 32), 0.0, A.mult, A.add)
        yield
        ts(v("hx0"), v("lf"), -8192.0, A.mult, 8192.0 - 2048.0, A.add)
        yield
        tt(v("s1"), v("cum"), v("p5", 32, 64), A.subtract)
        yield
        tt(v("OF"), v("s1"), v("pen"), A.max)
        yield
        cp(v("OFu"), v("OF"))
        yield

    def laid():
        ts(v("wl"), v("p5", 192, 224), 0.5, A.is_lt)
        yield
        tt(v("ld"), v("wl"), v("wm"), A.mult)
        yield
        tt(v("lo"), v("ld"), v("hm"), A.mult)
        yield
        tt(v("l2"), v("lo"), v("tc4096"), A.add)
        yield
        cp(v("lou"), v("l2"))
        yield

    def widths():
        ts(v("f3"), v("Ci"), 3, A.bitwise_and)
        tt(v("wv"), v("f3"), v("W4"), A.add)
        mm(v("p5", 64, 96), v("BD"), v("wv"))
        mm(v("p5", 96, 128), v("GE"), v("wv"))
        yield
        yield
        scan(v("cw"), v("on"), v("p5", 64, 96), 0.0, A.mult, A.add)
        tt(v("ee"), v("cw"), v("p5", 96, 128), A.subtract)
        tt(v("ec"), v("ee"), v("wv"), A.add)
        yield
        ts(v("fi"), v("ee"), 0.2, A.mult, 512.0, A.min)
        ts(v("nx"), v("ec"), 0.2, A.mult, 512.0, A.min)
        tt(v("mu"), v("nx"), v("fi"), A.subtract)
        yield
        ts(v("rc"), v("mu"), 0.5, A.is_ge)
        ts(v("pj"), v("mu"), 0.5, A.is_lt)
        tt(v("pj2"), v("pj"), v("tc512"), A.mult)
        tt(v("fo"), v("fi"), v("pj2"), A.max)
        cp(v("fou"), v("fo"))
        yield

    def slots():
        cp(ind(v("JW"), v("fou")), v("JV"))
        scan(v("JS"), v("JW", 0, 512), v("JW", 0, 512), -512.0, A.max, A.max)

    def slots_lists():
        to_list(v("p4", 0, 32), "JS")
        to_list(v("p4", 32, 64), "JW")

    def slots2():
        ts(v("jt"), v("p4", 32, 64), -256.5, A.is_lt, 512.0, A.mult)
        ts(v("JB"), v("p4", 0, 32), 768.0, A.add)
        tt(v("jj"), v("jt"), v("p4", 0, 32), A.add)
        ts(v("JJ"), v("jj"), 256.0, A.add)

    def numbers(t):
        act(v("NG"), ind(v("RB%d" % t, 96, 192), v("ngu")))
        yield
        to_list(v("p4", 96, 128), "NG")
        yield
        ts(v("n1"), v("p4", 96, 128), 0.5, A.is_ge)
        yield
        tt(v("n3"), v("n1"), v("n2"), A.mult)
        yield
        tt(v("n5"), v("n3"), v("n4"), A.mult)
        yield
        tt(v("Ci"), v("n5"), v("idx"), A.add)
        yield
        tt(v("Cf"), v("n5"), v("idx"), A.add)
        yield
        digits(v("Ci"), "dn")
        yield
        rows("dn")
        yield
        if t < R - 1:
            act(v("NW", 512, 1024), v("p6"))
        yield

    def put_numbers(t):
        act(v("YC"), v("p6"))
        dma("Y", "d3", T.yc[:, 512 * t:512 * t + 512], T.YC[2:128:16, :], [v("YC")], [])

    def u_fix(k, c):
        x = v("U", 1024 * k, 1024 * k + 1024)
        if k % 2:
            ts(x, x, col(c), A.add)
        else:
            act(x, x, AF.Identity, bias=col(c))
        return x

    def next_lists():
        to_list(v("p0", 0, 32), "NR")
        to_list(v("p0", 32, 64), "NR", 1)

    def gather(m):
        act(v("GS"), ind(v("U", 0, S), v("HL", 32 * m, 32 * m + 32)))

    def diff_of(m):
        o = 512 * (m % 2)
        return v("AB%d" % (m // 2 % 3), o, o + 512)

    def sum_up(k):
        bank = "p7" if k % 2 else "p2"
        for q in range(16):
            mm(v(bank, 64 * (k // 2), 64 * (k // 2) + 64), mat("FD", q), v("AB%d" % (k % 3), q, 1024, 16), q == 0, q == 15)

    def take(k):
        bank, o = "p7" if k % 2 else "p2", 64 * (k // 2)
        for j in (0, 1):
            act(v("KD2", 2 * k + j, 544, 17), v(bank, o + 32 * j, o + 32 * j + 32))

    def side(t):
        for x in (numbers(t - 1) if t else setup_last()):
            yield
        for x in widths():
            yield

    for t in range(R):
        last = t == R - 1
        lender, asker = T.cores[(rank + 1 + t) % 8], T.cores[(rank - 1 - t) % 8]
        cp(v("CL"), v("p0", 0, 64))
        if t == 0:
            cp(v("idx"), v("p0", 0, 32))
        else:
            tt(v("xt"), v("RB%d" % (t - 1), 96, 192), v("TS", 0, 96), A.mult)
            tt(v("Tw", S + 96 * t - 96, S + 96 * t), v("xt"), v("RB%d" % (t - 1), 0, 96), A.add)
        act(v("ZA"), ind(v("Tw", 0, W), v("CL", 0, 32)), AF.Identity, scale=col(0), bias=col(1))
        todo = side(t)
        if t:
            next(todo, None)
        tt(v("Z"), ind(v("Tw", 0, W), v("CL", 32, 64)), v("ZA"), A.min)
        if t == 0:
            setup_hash()
            for k in range(4):
                u_fix(k, 2)
            setup_fill()
        hash_sums("Z", NB)
        if t:
            next(todo, None)
        if t:
            weave(hash_uv(NB), (next(todo, None) for k in range(5)), 4)
        else:
            for x in hash_uv(NB):
                pass
        hash_lists(NB, "p1", 0, 8)
        hash_lists(NB, "p3", 8, 16)
        if t == 0:
            setup_late()
        else:
            next(todo, None)
        for x in lists("p1", 0, 0, 128):
            pass
        more = [lists("p3" if k > 1 else "p1", 128 * (k % 2), 128 * k, 128) for k in (1, 2, 3)]
        gather(SG[0])
        ready = []
        for i, m in enumerate([m for m in range(16) if m not in SG]):
            df = "DF%d" % (i % 3)
            tt(v(df), ind(v("U", 0, S), v("HL", 32 * m, 32 * m + 32)), v("Z"), A.subtract)
            act(diff_of(m), v(df), AF.Abs)
            for k in ready:
                take(k)
            ready = []
            done = [m // 2] if m % 2 else []
            if m + 1 in SG:
                mm(v("p4"), v("ID"), v("GS"), True, False)
                mm(v("p4"), v("NI"), v("Z"), False, True)
                act(diff_of(m + 1), v("p4"), AF.Abs)
                done = [m // 2]
            if i < 9:
                next(more[i // 3])
            if i == 6:
                gather(SG[1])
            if i >= 1:
                next(todo, None)
            for k in done:
                sum_up(k)
                ready.append(k)
        for x in todo:
            pass
        for k in ready:
            take(k)
        slots()
        scan(v("KAB", 0, 544), v("DA"), v("KD2"), 0.0, A.add, A.min)
        scan(v("KAB", 544, 1088), v("DB"), v("KD2"), 0.0, A.add, A.min)
        weave(best(NB, v("KAB", 16, 1088, 17)), poor())
        tt(v("hh"), v("hx0"), v("Hh"), A.add)
        tt(v("hx"), v("hx0"), v("Hh"), A.add)
        for q in range(16):
            mm(v("p1", q, 512, 16), mat("E1", q), v("hh"))
        cp(ind(v("ZS"), v("OFu")), v("Z"))
        send("az%d" % t, "lz", lender, T["ZR%d" % t][:, :], T.ZS[:, 0:96], [v("ZS", 0, 96)])
        mm(v("p7"), v("ZM"), v("Z"), True, False)
        ts(v("hc"), v("hx"), 2048.0, A.add)
        cp(v("wm", 0, NS), v("lf", 0, NS))
        tt(v("hm"), v("Hh"), v("tc4096"), A.subtract)
        tt(v("a1"), v("Hh"), v("Cf"), A.subtract)
        if not last:
            act(v("TC"), ind(v("Tw", 0, W), v("CL", 0, 32)))
        if t:
            put_numbers(t - 1)
        ts(v("HR"), v("p1"), 2048.0, A.add)
        for b in range(NS, NB):
            e = 512 * b
            ts(v("EQ", e - 16 * b, e + 16), v("HR", 0, 16 * b + 16), v("hc", b, b + 1), A.is_equal)
            add_up(v("LJ", 0, 16 * b), v("EQ", e - 16 * b, e), v("la", b, b + 1))
        for b in range(NS):
            e, w = 512 * b, 16 * NS - 16 * b
            ts(v("EQ", e, e + w), v("HR", 16 * b, 16 * NS), v("hc", b, b + 1), A.is_equal)
            if b < NS - 1:
                mm(v("p7", 16 * b + 16, 16 * NS), v("BD"), v("EQ", e + 16, e + w), False, False)
        for q in range(1, 16):
            mm(v("p7", q, 512, 16), mat("LQ", q), v("EQ", q, 15872 + q + 1, 512), False, q == 15)
        act(v("LS"), v("p7"))
        zr = "ZR%d" % t
        for k in range(4):
            act(v("z4", 96 * k, 96 * k + 96), v(zr))
        hash_sums(zr, NA)
        to_list(v("p5", 192, 224), "LS")
        if not last:
            mm(v("p5", 224, 225), v("O16"), v("cum", 31, 32))
        slots_lists()
        if not last:
            cp(ind(v("TS"), v("OFu")), v("TC"))
        ts(v("wn", NS, NB), v("la", NS, NB), 0.5, A.is_lt)
        tt(v("wm", NS, NB), v("wn", NS, NB), v("lf", NS, NB), A.mult)
        weave(hash_uv(NA), laid(), 4)
        hash_lists(NA, "p1", 0, 16)
        cp(ind(v("U", 0, ZC), v("lou")), v("L255"))
        if not last:
            cp(v("Pi"), v("p5", 224, 225))
        for x in lists("p1", 0, 0, 96):
            pass
        for k in range(4):
            df, ab, o = "DF%d" % (k % 3), "AB%d" % (k // 2), 384 * (k % 2)
            tt(v(df, 0, 384), ind(v("U", 0, S), v("HL", 24 * k, 24 * k + 24)), v("z4"), A.subtract)
            act(v(ab, o, o + 384), v(df, 0, 384), AF.Abs)
            if k % 2:
                for q in range(16):
                    mm(v("p2", 48 * (k // 2), 48 * (k // 2) + 48), mat("FD", q), v(ab, q, 768, 16), q == 0, q == 15)
        for b in range(NA):
            act(v("KE", 17 * b, 17 * b + 16), v("p2", b, 96, NA))
        tt(v("a2"), v("a1"), v("ld"), A.mult)
        ts(v("a3"), v("OF"), 95.5, A.is_lt)
        ts(v("a4"), v("OF"), float(S + 96 * t), A.add)
        tt(v("a5"), v("a4"), v("Cf"), A.subtract)
        tt(v("a7"), v("a2"), v("Cf"), A.add)
        tt(v("a6"), v("a5"), v("a3"), A.mult)
        tt(v("Ai"), v("a7"), v("a6"), A.add)
        digits(v("Ai"))
        rows("dh")
        slots2()
        act(v("NW", 0, 512), v("p6"))
        act(v("NR", 0, 512), ind(v("NW"), v("JJ")))
        scan(v("KAB", 0, 102), v("DA", 0, 102), v("KE"), 0.0, A.add, A.min)
        scan(v("KAB", 102, 204), v("DB", 0, 102), v("KE"), 0.0, A.add, A.min)
        key = v("KAB", 16, 102, 17)

        def fits():
            ts(v("k6", 0, NA), key, col(10), A.is_ge, 8192.0, A.mult)
            yield
            ts(v("gt", 0, NA), key, col(10), A.is_lt)
            yield
        weave(best(NA, v("KAB", 16, 204, 17)), fits(), 1)
        ts(v("k7", 0, NA), v("Hh", 0, NA), -2048.0, A.add)
        tt(v("ha"), v("k6", 0, NA), v("k7", 0, NA), A.add)
        for q in range(16):
            mm(v("p1", q, 96, 16), mat("E1", q), v("ha"))
        next_lists()
        ts(v("gh", 0, NA), v("Hh", 0, NA), float(-ZC), A.add)
        tt(v("gn", 0, NA), v("Hh", 0, NA), v("tc4096", 0, NA), A.subtract)
        tt(v("Hd"), v("p1", 0, 96), v("msk"), A.add)
        for b in range(NA):
            if b:
                ts(v("EA", 96 * b, 96 * b + 16 * b), v("p1", 0, 16 * b), v("k7", b, b + 1), A.is_equal)
            ts(v("EA", 112 * b, 112 * b + 16), v("Hd", 16 * b, 16 * b + 16), v("k7", b, b + 1), A.is_equal)
            add_up(v("Hj", 0, 16 * b + 16), v("EA", 96 * b, 112 * b + 16), v("la", 32 + b, 33 + b))
        ts(v("gm0", 0, NA), v("la", 32, 32 + NA), 0.5, A.is_lt)
        tt(v("gm", 0, NA), v("gm0", 0, NA), v("gt", 0, NA), A.mult)
        tt(v("gl", 0, NA), v("gm", 0, NA), v("gh", 0, NA), A.mult)
        ts(v("glu", 0, NA), v("gl", 0, NA), float(ZC), A.add)
        act(v("SB", 96, 192), ind(v("FL"), v("glu", 0, NA)))
        cp(v("SB", 0, 96), ind(v("Tw"), v("glu", 0, NA)))
        send("ar%d" % t, "ly", asker, T["RB%d" % t][:, :], T.SB[:, :], [v("SB")])
        act(v("SU"), ind(v("U"), v("glu", 0, NA)))
        send("au%d" % t, "lx", asker, T.UP[:, 96 * t:96 * t + 96], T.SU[:, :], [v("SU")])
        act(v("NB2"), ind(v("NW"), v("JB")))
        if not last:
            act(v("JW"), v("JP"))
        to_list(v("p4", 64, 96), "NB2")
        tt(v("go", 0, NA), v("gn", 0, NA), v("gm", 0, NA), A.mult)
        tt(v("gp", 0, NA), v("go", 0, NA), v("tc4096", 0, NA), A.add)
        cp(v("sou", 0, NA), v("gp", 0, NA))
        cp(ind(v("U", 0, ZC), v("sou", 0, NA)), v("L255", 0, 96))
        if not last:
            ts(v("Pj"), v("Pi"), 63, A.bitwise_and)
            tt(col(16), col(9), v("Pj"), A.add)
            ts(col(10), col(16), 4081.0, A.min, 4096.0, A.mult)
            ms(v("ZS", 0, 96), 1024.0)
        base = float(S + 96 * t)
        cp(v("idx"), v("p0", 0, 32))
        ts(v("ngu"), v("idx"), -base, A.add, 0.0, A.max)
        ts(v("n2"), v("idx"), base, A.is_ge)
        if last:
            for k in range(4):
                x = u_fix(k, 3)
                dma("Y", "d4", T.yu[:, 1024 * k:1024 * k + 1024], x[0], [x], [])
        tt(v("n4"), v("p4", 64, 96), v("idx"), A.subtract)

    for x in numbers(R - 1):
        pass
    put_numbers(R - 1)
    ts(v("UP"), v("UP"), col(3), A.add)
    dma("Y", "d5", T.yu[:, S:W], T.UP[:, :], [v("UP")], [])
    for e, n in sorted(count.items()):
        g.wait_ge(T.sem[SEM.get(e, e[1:])], n)
